import numpy as np
import ml_dtypes


def mxq(x, axis, fmt="e4m3"):
    dtype, down = {"e4m3": (ml_dtypes.float8_e4m3fn, 7), "e5m2": (ml_dtypes.float8_e5m2, 14)}[fmt]
    v = np.moveaxis(np.asarray(x, np.float32).astype(ml_dtypes.bfloat16).astype(np.float64), axis, -1)
    blocks = v.reshape(v.shape[:-1] + (-1, 32))
    amax = np.abs(blocks).max(-1, keepdims=True)
    byte = np.maximum(np.where(amax > 0, np.frexp(amax)[1] - 1 + 127, 0) - down, 1)
    scale = np.exp2(byte - 127.0)
    codes = (blocks / scale).astype(np.float32).astype(dtype).astype(np.float64)
    return np.moveaxis((codes * scale).reshape(v.shape), -1, axis)


WIDE = False


def mx_kscale(k):
    if not WIDE:
        return np.ones(k)
    levels = np.array([10, -10, 5, -5, 0])
    if k % 512:
        return np.exp2(np.random.permutation(np.resize(levels, k // 32))).repeat(32)
    a = np.empty((k // 512, 16))
    for p in range(k // 512):
        a[p, :8] = np.random.permutation(np.resize(levels, 8))
        for g in range(8):
            far = levels[np.abs(levels - a[p, g]) >= 10]
            a[p, g + 8] = far[np.random.randint(len(far))]
    return np.exp2(a.ravel()).repeat(32)


BF16 = ml_dtypes.bfloat16


def bf(x):
    return np.asarray(x, np.float32).astype(BF16)


def f64(x):
    return np.asarray(x).astype(np.float64)


E2M1 = np.array([0.0, 0.5, 1.0, 1.5, 2.0, 3.0, 4.0, 6.0, -0.0, -0.5, -1.0, -1.5, -2.0, -3.0, -4.0, -6.0])


def pack_weight(w, fmt):
    k, n = w.shape
    w = f64(bf(w)).reshape(k // 32, 32, n)
    amax = np.abs(w).max(1)
    if fmt == "e4m3":
        byte = np.frexp(amax)[1] - 1 + 127 - 7
    else:
        mant, ex = np.frexp(amax / 6.0)
        byte = np.where(mant > 0.5, ex, ex - 1) + 127
    byte = np.clip(np.where(amax > 0, byte, 1), 1, 254)
    scaled = (w * np.exp2(127.0 - byte)[:, None, :]).reshape(k, n).astype(np.float32)
    by_word = np.ascontiguousarray(scaled.reshape(k // 512, 128, 4, n).transpose(0, 1, 3, 2))
    if fmt == "e4m3":
        words = by_word.astype(ml_dtypes.float8_e4m3fn).view(np.uint8)
    else:
        c = by_word.astype(ml_dtypes.float4_e2m1fn).view(np.uint8) & 0xF
        words = c[..., 0::2] | (c[..., 1::2] << 4)
    return np.ascontiguousarray(words), np.ascontiguousarray(byte.astype(np.uint8).reshape(k // 512, 16, n))


def unpack_weight(words, scales, fmt):
    g, p, n, _ = words.shape
    if fmt == "e4m3":
        vals = np.ascontiguousarray(words).view(ml_dtypes.float8_e4m3fn).astype(np.float64)
    else:
        nib = np.empty((g, p, n, 4), np.uint8)
        nib[..., 0::2] = words & 0xF
        nib[..., 1::2] = words >> 4
        vals = E2M1[nib]
    vals = vals * np.repeat(np.exp2(scales.astype(np.float64) - 127.0), 8, axis=1)[..., None]
    return vals.transpose(0, 1, 3, 2).reshape(g * 512, n)
def pack4(w):
    words, scales = pack_weight(w, "e2m1")
    return words.reshape(words.shape[0], 128, -1), scales


def unpack4(words, scales):
    return unpack_weight(words.reshape(words.shape[0], 128, -1, 2), scales, "e2m1")


def planes(Y):
    n, m = Y.shape
    b = f64(bf(Y)).reshape(n // 32, 32, m)
    amax = np.abs(b).max(1)
    byte = np.clip(np.where(amax > 0, np.frexp(amax)[1] - 1 + 127 - 7, 1), 1, 254)
    codes = (b * np.exp2(127.0 - byte)[:, None, :]).reshape(n, m).astype(np.float32).astype(ml_dtypes.float8_e4m3fn).view(np.uint8)
    words = codes.reshape(n // 512, 128, 4, m).transpose(0, 1, 3, 2)
    return np.ascontiguousarray(words), np.ascontiguousarray(byte.astype(np.uint8).reshape(n // 512, 16, m))


M, I, J, N = 1024, 32, 64, 1536
K = I * J

def setup_inputs():
    s = mx_kscale(K)
    a = bf(1.5 * np.random.randn(M, I))
    b = bf(1.5 * np.random.randn(M, J))
    lam = bf(np.exp(0.3 * np.random.randn(K)) * s)
    core = np.random.randn(K, N) * 2.0 / np.sqrt(K)
    core_words, core_scales = pack4(core / s[:, None])
    beta = bf(0.4 * np.random.randn(N))
    spread = np.exp(0.8 * np.random.randn(N))
    gamma = bf(spread)
    h = bf(0.6 * np.random.randn(M, N) * spread)
    return {"a": a, "b": b, "lam": lam, "core_words": core_words, "core_scales": core_scales,
            "beta": beta, "gamma": gamma, "h": h}

def reference(a, b, lam, core_words, core_scales, beta, gamma, h):
    u = np.tanh(f64(a))
    v = np.tanh(f64(b))
    phi = (u[:, :, None] * v[:, None, :]).reshape(M, K) * f64(lam)
    W = unpack4(core_words, core_scales)
    P = mxq(phi, 1, "e4m3") @ W
    y = f64(h) + f64(gamma) * np.tanh(P + f64(beta))
    Y = y.T
    words, scales = planes(Y)
    return y, words, scales

@@ -1,0 +1,344 @@
+from contextlib import ExitStack
+
+import concourse.mybir as mybir
+from concourse.masks import make_identity
+
+M, I, J, N = 1024, 32, 64, 1536
+K = I * J
+FLOPS = 2 * M * K * N
+
+F32 = mybir.dt.float32
+BF16 = mybir.dt.bfloat16
+I32 = mybir.dt.int32
+U32 = mybir.dt.uint32
+U8 = mybir.dt.uint8
+FP8X4 = mybir.dt.float8_e4m3fn_x4
+FP4X4 = mybir.dt.float4_e2m1fn_x4
+ACT = mybir.ActivationFunctionType
+ALU = mybir.AluOpType
+
+P = 128
+CHUNK = 512
+CHUNKS = M // CHUNK
+TT = CHUNK // P
+PASSES = K // 512
+FT = N // P
+FG = N // 512
+
+
+def tile_tucker_fusion_planes_g4_kernel(
+    tc, a, b, lam, core_words, core_scales, beta, gamma, h, out_0, out_1, out_2
+):
+    nc = tc.nc
+    with ExitStack() as ctx:
+        keep = ctx.enter_context(tc.tile_pool(name="keep", bufs=1))
+        work = ctx.enter_context(tc.tile_pool(name="work", bufs=3))
+        psum = ctx.enter_context(tc.psum_pool(name="psum", bufs=1))
+        ctx.enter_context(tc.manual_schedule())
+
+        def bank(tag, dtype=F32):
+            return psum.tile([P, 512], dtype, name=tag, tag=tag)
+
+        lam_words = keep.tile([P, 8], F32)
+        a_sb = keep.tile([P, CHUNKS, TT * I], BF16)
+        b_sb = keep.tile([P, CHUNKS, TT * J], BF16)
+        w_scales = keep.tile([P, PASSES, N], U8, align_bytes=64)
+        w_words = keep.tile([P, PASSES, 2 * N], U8, align_bytes=64)
+        rows = keep.tile([P, P], BF16)
+        h_sb = keep.tile([P, CHUNKS, TT, N], BF16)
+        warm = keep.tile([P, 1], F32)
+        warm_out = keep.tile([P, 1], F32)
+        ident = keep.tile([P, P], F32)
+        ident_bf = keep.tile([P, P], BF16)
+        perm = keep.tile([P, P], F32)
+
+        with nc.allow_non_contiguous_dma(reason="one 4-byte pair of lam to a partition"):
+            nc.sync.dma_start(out=lam_words[:], in_=lam.bitcast(F32).rearrange("(r q) -> q r", q=P))
+        nc.sync.dma_start(out=b_sb[:], in_=b.rearrange("(c m t) j -> m c (t j)", c=CHUNKS, t=TT))
+        nc.sync.dma_start(out=a_sb[:], in_=a.rearrange("(c m t) i -> m c (t i)", c=CHUNKS, t=TT))
+
+        nc.vector.memset(warm[:], 0.0)
+        nc.scalar.activation(out=warm_out[:], in_=warm[:], func=ACT.Tanh)
+        make_identity(nc, ident[:])
+        nc.vector.memset(w_scales[:].rearrange("p g n -> p (g n)").bitcast(I32), 0)
+        nc.vector.memset(rows[:], 0.0)
+        nc.vector.tensor_copy(
+            out=perm[:].rearrange("q (i u c) -> q i u c", i=4, u=2),
+            in_=ident[:].rearrange("q (i c u) -> q i u c", i=4, u=2),
+        )
+        nc.vector.tensor_copy(out=ident_bf[:], in_=ident[:])
+
+        for q in range(4):
+            nc.sync.dma_start(
+                out=w_scales[32 * q : 32 * q + 4, :, :].bitcast(I32),
+                in_=core_scales[:, 4 * q : 4 * q + 4, :].rearrange("g r n -> r g n").bitcast(I32),
+            )
+        for g in range(PASSES):
+            nc.sync.dma_start(out=w_words[:, g, :].bitcast(I32), in_=core_words[g].bitcast(I32))
+        nc.sync.dma_start(out=rows[0:FT, :], in_=beta.rearrange("(j p) -> j p", p=P))
+        nc.sync.dma_start(out=rows[FT : 2 * FT, :], in_=gamma.rearrange("(j p) -> j p", p=P))
+        for c in range(CHUNKS):
+            nc.sync.dma_start(
+                out=h_sb[:, c, :, :],
+                in_=h[CHUNK * c : CHUNK * (c + 1), :].rearrange("(m t) n -> m t n", t=TT),
+            )
+
+        lam_ps = []
+        for half in range(2):
+            lam_bank = bank("l%d" % half)
+            for r in range(4):
+                col = 4 * half + r
+                nc.tensor.transpose(
+                    lam_bank[:, P * r : P * (r + 1)], lam_words[:, col : col + 1].to_broadcast([P, P]), perm[:]
+                )
+            lam_ps.append(lam_bank)
+
+        u_sb = keep.tile([P, CHUNKS, TT * I], F32)
+        v_sb = keep.tile([P, CHUNKS, 2, TT, 32], F32)
+
+        def factors(c):
+            nc.scalar.activation(
+                out=v_sb[:, c].rearrange("m u t (c e) -> m u (t c) e", e=2),
+                in_=b_sb[:, c, :].rearrange("m (x u e) -> m u x e", u=2, e=2),
+                func=ACT.Tanh,
+            )
+            nc.scalar.activation(out=u_sb[:, c, :], in_=a_sb[:, c, :], func=ACT.Tanh)
+
+        factors(0)
+        factors(1)
+
+        turn = [0]
+
+        def turn_bank(dtype=F32):
+            turn[0] += 1
+            return bank("t%d" % (turn[0] % 2), dtype)
+
+        phi_tok, phi_k, codes, scales = {}, {}, {}, {}
+
+        def products(n, hf):
+            c, g = divmod(n, PASSES)
+            if hf == 0:
+                phi_tok[n] = work.tile([P, TT, 2, 256], BF16, name="phi_tok", tag="phi_tok")
+            for t in (2 * hf, 2 * hf + 1):
+                for ii in range(8):
+                    i = 8 * g + ii
+                    lam_i = lam_ps[i // 16][:].bitcast(BF16)[:, 64 * (i % 16) : 64 * (i % 16 + 1)]
+                    nc.vector.scalar_tensor_tensor(
+                        out=phi_tok[n][:, t, :, 32 * ii : 32 * (ii + 1)],
+                        in0=lam_i.rearrange("m (u x) -> m u x", u=2),
+                        scalar=u_sb[:, c, I * t + i : I * t + i + 1],
+                        in1=v_sb[:, c, :, t, :],
+                        op0=ALU.mult,
+                        op1=ALU.mult,
+                    )
+
+        def turn_phi(n, hf):
+            if hf == 0:
+                phi_k[n] = work.tile([P, CHUNK * 4], BF16, name="phi_k", tag="phi_k", align_bytes=64)
+            ps = turn_bank()
+            for s in range(2):
+                for u in range(2):
+                    nc.tensor.transpose(
+                        ps[:, P * (2 * s + u) : P * (2 * s + u + 1)],
+                        phi_tok[n][:, 2 * hf + s, u, :].bitcast(F32),
+                        ident[:],
+                    )
+            nc.scalar.copy(
+                out=phi_k[n][:, 1024 * hf : 1024 * (hf + 1)].bitcast(F32).rearrange("p (s m u) -> p s m u", s=2, u=2),
+                in_=ps[:].rearrange("p (s u m) -> p s m u", s=2, u=2),
+            )
+
+        def quantize_phi(n):
+            codes[n] = keep.tile([P, CHUNK], U32, name="codes%d" % n, align_bytes=64)
+            scales[n] = keep.tile([P, CHUNK], U8, name="scales%d" % n, align_bytes=64)
+            nc.vector.quantize_mx(out=codes[n][:].bitcast(FP8X4), scales=scales[n][:], in_=phi_k[n][:])
+
+        acc = {}
+
+        def mx_pass(c, j, g, tag):
+            if g == 0:
+                acc[(c, j)] = bank(tag)
+            n = PASSES * c + g
+            nc.tensor.matmul_mx(
+                out=acc[(c, j)][:],
+                lhsT=w_words[:, g, 2 * P * j : 2 * P * (j + 1)].bitcast(FP4X4),
+                lhsT_scale=w_scales[:, g, P * j : P * (j + 1)],
+                rhs=codes[n][:].bitcast(FP8X4),
+                rhs_scale=scales[n][:],
+                start=(g == 0),
+                stop=(g == PASSES - 1),
+            )
+
+        cols = keep.tile([P, 2 * FT], F32)
+
+        def turn_rows():
+            ps = turn_bank(BF16)
+            nc.tensor.transpose(ps[:, 0:P], rows[:], ident_bf[:])
+            nc.scalar.copy(out=cols[:], in_=ps[:, 0 : 2 * FT])
+
+        bounded, gained = {}, {}
+
+        def bound(c, j):
+            bounded[(c, j)] = work.tile([P, CHUNK], F32, name="bounded", tag="bounded", bufs=4)
+            nc.scalar.activation(out=bounded[(c, j)][:], in_=acc[(c, j)][:], func=ACT.Tanh, bias=cols[:, j : j + 1])
+
+        def gain(c, j, engine):
+            gained[(c, j)] = work.tile([P, CHUNK], F32, name="gained", tag="gained", bufs=14)
+            g_col = cols[:, FT + j : FT + j + 1]
+            if engine == "scalar":
+                nc.scalar.activation(out=gained[(c, j)][:], in_=bounded[(c, j)][:], func=ACT.Copy, scale=g_col)
+            else:
+                eng = nc.vector if engine == "vector" else nc.gpsimd
+                eng.tensor_scalar(
+                    out=gained[(c, j)][:], in0=bounded[(c, j)][:], scalar1=g_col, scalar2=0.0,
+                    op0=ALU.mult, op1=ALU.add,
+                )
+
+        y, y_pairs, y_k = {}, {}, {}
+        back = {}
+
+        def turn_gained(c, j, tag):
+            back[(c, j)] = bank(tag)
+            for t in range(TT):
+                nc.tensor.transpose(
+                    back[(c, j)][:, P * t : P * (t + 1)], gained[(c, j)][:, P * t : P * (t + 1)], ident[:]
+                )
+
+        def add_stream(c, j):
+            f, jj = divmod(j, 4)
+            if jj == 0:
+                y[(c, f)] = work.tile([P, TT, 512], F32, name="y", tag="y", bufs=4)
+            nc.vector.tensor_tensor(
+                out=y[(c, f)][:, :, P * jj : P * (jj + 1)],
+                in0=back[(c, j)][:].rearrange("m (t p) -> m t p", t=TT),
+                in1=h_sb[:, c, :, P * j : P * (j + 1)],
+                op=ALU.add,
+            )
+
+        def store_y(c, f, lo, hi):
+            dst = out_0[CHUNK * c : CHUNK * (c + 1), 512 * f + lo : 512 * f + hi]
+            nc.sync.dma_start(out=dst.rearrange("(m t) n -> m t n", t=TT), in_=y[(c, f)][:, :, lo:hi])
+
+        def round_y(c, f, lo, hi):
+            if lo == 0:
+                y_pairs[(c, f)] = work.tile([P, 2, TT, 256], BF16, name="y_pairs", tag="y_pairs")
+            nc.vector.tensor_copy(
+                out=y_pairs[(c, f)][:, :, :, lo // 2 : hi // 2].rearrange("m u t (p e) -> m u t p e", e=2),
+                in_=y[(c, f)][:, :, lo:hi].rearrange("m t (p u e) -> m u t p e", u=2, e=2),
+            )
+
+        def turn_y(c, f, engines):
+            y_k[(c, f)] = work.tile([P, CHUNK * 4], BF16, name="y_k", tag="y_k", align_bytes=64)
+            words = y_k[(c, f)][:].bitcast(F32).rearrange("p (m t u) -> p m t u", t=TT, u=2)
+            for hf in range(2):
+                ps = turn_bank()
+                for s in range(2):
+                    for u in range(2):
+                        nc.tensor.transpose(
+                            ps[:, P * (2 * s + u) : P * (2 * s + u + 1)],
+                            y_pairs[(c, f)][:, u, 2 * hf + s, :].bitcast(F32),
+                            ident[:],
+                        )
+                dst = words[:, :, 2 * hf : 2 * hf + 2, :]
+                src = ps[:].rearrange("p (s u m) -> p m s u", s=2, u=2)
+                if engines[hf] == "scalar":
+                    nc.scalar.copy(out=dst, in_=src)
+                else:
+                    nc.vector.tensor_copy(out=dst, in_=src)
+
+        y_scales = keep.tile([P, FG, M], U8, align_bytes=64)
+
+        def quantize_y(c, f):
+            y_codes = work.tile([P, CHUNK], U32, name="y_codes", tag="y_codes", align_bytes=64)
+            nc.vector.quantize_mx(
+                out=y_codes[:].bitcast(FP8X4),
+                scales=y_scales[:, f, CHUNK * c : CHUNK * (c + 1)],
+                in_=y_k[(c, f)][:],
+            )
+            dst = out_1[f].rearrange("p m t -> p (m t)")[:, 4 * CHUNK * c : 4 * CHUNK * (c + 1)]
+            nc.sync.dma_start(out=dst.bitcast(I32), in_=y_codes[:].bitcast(I32))
+
+        early = ("x0", "x1", "x2", "x3")
+        for n in range(PASSES + 1):
+            products(n, 0)
+            if n < PASSES:
+                turn_phi(n, 0)
+            if n > 0:
+                quantize_phi(n - 1)
+                for j in range(4):
+                    mx_pass(0, j, n - 1, early[j])
+            if n == 2:
+                turn_rows()
+            if n < PASSES:
+                products(n, 1)
+                turn_phi(n, 1)
+        for j in range(4):
+            bound(0, j)
+            gain(0, j, "gpsimd")
+
+        def mx_pair(k, engine):
+            c, kk = divmod(k, FT // 2)
+            for s in range(2):
+                for g in range(PASSES):
+                    mx_pass(c, 2 * kk + s, g, "x%d" % s)
+                bound(c, 2 * kk + s)
+            for s in range(2):
+                gain(c, 2 * kk + s, engine)
+
+        for n in range(PASSES, 2 * PASSES):
+            if n > PASSES:
+                products(n, 0)
+                if n > PASSES + 1:
+                    add_stream(0, n - PASSES - 2)
+                quantize_phi(n - 1)
+            products(n, 1)
+            turn_phi(n, 0)
+            turn_phi(n, 1)
+            if n > PASSES:
+                turn_gained(0, n - PASSES - 1, "x%d" % (2 + n % 2))
+            mx_pair(n - 2, "gpsimd")
+        add_stream(0, 2)
+        quantize_phi(2 * PASSES - 1)
+
+        back_tags = ("l0", "l1", "x2", "x3")
+        runs = [
+            ([(0, 3), (0, 4), (0, 5), (0, 6)], None),
+            ([(0, 7), (0, 8), (0, 9), (0, 10)], (0, 0)),
+            ([(0, 11), (1, 0), (1, 1)], (0, 1)),
+            ([(1, 2), (1, 3)], (0, 2)),
+            ([(1, 4), (1, 5)], (1, 0)),
+            ([(1, 6), (1, 7)], None),
+            ([(1, 8), (1, 9)], (1, 1)),
+        ]
+        for step, (tiles, plane) in enumerate(runs):
+            if step > 0:
+                mx_pair(5 + step, "scalar" if step < len(runs) - 1 else "vector")
+            for s, (c, j) in enumerate(tiles):
+                turn_gained(c, j, back_tags[s])
+            if plane is not None:
+                turn_y(plane[0], plane[1], ("scalar", "scalar"))
+            for c, j in tiles:
+                add_stream(c, j)
+            for c, j in tiles:
+                if j % 4 == 3:
+                    round_y(c, j // 4, 0, 512)
+                    store_y(c, j // 4, 0, 512)
+            if step == len(runs) - 1:
+                round_y(1, 2, 0, 256)
+                store_y(1, 2, 0, 256)
+            if plane is not None:
+                quantize_y(plane[0], plane[1])
+        for j in (10, 11):
+            turn_gained(1, j, back_tags[j % 4])
+        for j in (10, 11):
+            add_stream(1, j)
+        round_y(1, 2, 256, 512)
+        store_y(1, 2, 256, 512)
+        turn_y(1, 2, ("scalar", "vector"))
+        quantize_y(1, 2)
+        for q in range(4):
+            eng = nc.sync if q % 2 == 0 else nc.scalar
+            eng.dma_start(
+                out=out_2[:, 4 * q : 4 * q + 4, :].rearrange("f r m -> r f m").bitcast(I32),
+                in_=y_scales[32 * q : 32 * q + 4, :, :].bitcast(I32),
+            )

@@ -39,9 +39,10 @@ def tile_tucker_fusion_planes_g4_kernel(
         def bank(tag, dtype=F32):
             return psum.tile([P, 512], dtype, name=tag, tag=tag)
 
+        lam_rows = keep.tile([P, P], F32)
         lam_words = keep.tile([P, 8], F32)
-        a_sb = keep.tile([P, CHUNKS, TT * I], BF16)
-        b_sb = keep.tile([P, CHUNKS, TT * J], BF16)
+        a_sb = keep.tile([P, CHUNKS, TT, I], BF16)
+        b_sb = keep.tile([P, CHUNKS, TT, J], BF16)
         w_scales = keep.tile([P, PASSES, N], U8, align_bytes=64)
         w_words = keep.tile([P, PASSES, 2 * N], U8, align_bytes=64)
         rows = keep.tile([P, P], BF16)
@@ -52,16 +53,21 @@ def tile_tucker_fusion_planes_g4_kernel(
         ident_bf = keep.tile([P, P], BF16)
         perm = keep.tile([P, P], F32)
 
-        with nc.allow_non_contiguous_dma(reason="one 4-byte pair of lam to a partition"):
-            nc.sync.dma_start(out=lam_words[:], in_=lam.bitcast(F32).rearrange("(r q) -> q r", q=P))
-        nc.sync.dma_start(out=b_sb[:], in_=b.rearrange("(c m t) j -> m c (t j)", c=CHUNKS, t=TT))
-        nc.sync.dma_start(out=a_sb[:], in_=a.rearrange("(c m t) i -> m c (t i)", c=CHUNKS, t=TT))
+        order = ("(m t)", "(t m)")
+
+        def tokens(ap, c):
+            return ap[CHUNK * c : CHUNK * (c + 1), :].rearrange(order[c] + " n -> m t n", t=TT)
+
+        nc.vector.memset(lam_rows[:], 0.0)
+        nc.sync.dma_start(out=lam_rows[0:8, :], in_=lam.bitcast(F32).rearrange("(r q) -> r q", q=P))
+        nc.sync.dma_start(out=b_sb[:, 0], in_=tokens(b, 0))
+        nc.sync.dma_start(out=a_sb[:, 0], in_=tokens(a, 0))
 
         nc.vector.memset(warm[:], 0.0)
         nc.scalar.activation(out=warm_out[:], in_=warm[:], func=ACT.Tanh)
         make_identity(nc, ident[:])
-        nc.vector.memset(w_scales[:].rearrange("p g n -> p (g n)").bitcast(I32), 0)
         nc.vector.memset(rows[:], 0.0)
+        nc.vector.memset(w_scales[:].rearrange("p g n -> p (g n)").bitcast(I32), 0)
         nc.vector.tensor_copy(
             out=perm[:].rearrange("q (i u c) -> q i u c", i=4, u=2),
             in_=ident[:].rearrange("q (i c u) -> q i u c", i=4, u=2),
@@ -73,15 +79,27 @@ def tile_tucker_fusion_planes_g4_kernel(
                 out=w_scales[32 * q : 32 * q + 4, :, :].bitcast(I32),
                 in_=core_scales[:, 4 * q : 4 * q + 4, :].rearrange("g r n -> r g n").bitcast(I32),
             )
-        for g in range(PASSES):
-            nc.sync.dma_start(out=w_words[:, g, :].bitcast(I32), in_=core_words[g].bitcast(I32))
-        nc.sync.dma_start(out=rows[0:FT, :], in_=beta.rearrange("(j p) -> j p", p=P))
-        nc.sync.dma_start(out=rows[FT : 2 * FT, :], in_=gamma.rearrange("(j p) -> j p", p=P))
-        for c in range(CHUNKS):
+        for f in range(FG):
             nc.sync.dma_start(
-                out=h_sb[:, c, :, :],
-                in_=h[CHUNK * c : CHUNK * (c + 1), :].rearrange("(m t) n -> m t n", t=TT),
+                out=w_words[:, :, 1024 * f : 1024 * (f + 1)].bitcast(I32),
+                in_=core_words[:, :, 1024 * f : 1024 * (f + 1)].rearrange("g p n -> p g n").bitcast(I32),
             )
+        nc.gpsimd.dma_start(out=rows[0:FT, :], in_=beta.rearrange("(j p) -> j p", p=P))
+        nc.gpsimd.dma_start(out=rows[FT : 2 * FT, :], in_=gamma.rearrange("(j p) -> j p", p=P))
+        nc.sync.dma_start(out=b_sb[:, 1], in_=tokens(b, 1))
+        nc.sync.dma_start(out=a_sb[:, 1], in_=tokens(a, 1))
+        for c in range(CHUNKS):
+            nc.sync.dma_start(out=h_sb[:, c], in_=tokens(h, c))
+
+        turn = [0]
+
+        def turn_bank(dtype=F32):
+            turn[0] += 1
+            return bank("t%d" % (turn[0] % 2), dtype)
+
+        ps = turn_bank()
+        nc.tensor.transpose(ps[:, 0:P], lam_rows[:], ident[:])
+        nc.vector.tensor_copy(out=lam_words[:], in_=ps[:, 0:8])
 
         lam_ps = []
         for half in range(2):
@@ -93,81 +111,94 @@ def tile_tucker_fusion_planes_g4_kernel(
                 )
             lam_ps.append(lam_bank)
 
-        u_sb = keep.tile([P, CHUNKS, TT * I], F32)
+        u_sb = keep.tile([P, CHUNKS, TT, I], F32)
         v_sb = keep.tile([P, CHUNKS, 2, TT, 32], F32)
 
         def factors(c):
             nc.scalar.activation(
                 out=v_sb[:, c].rearrange("m u t (c e) -> m u (t c) e", e=2),
-                in_=b_sb[:, c, :].rearrange("m (x u e) -> m u x e", u=2, e=2),
+                in_=b_sb[:, c].rearrange("m t (x u e) -> m u (t x) e", u=2, e=2),
                 func=ACT.Tanh,
             )
-            nc.scalar.activation(out=u_sb[:, c, :], in_=a_sb[:, c, :], func=ACT.Tanh)
-
-        factors(0)
-        factors(1)
-
-        turn = [0]
-
-        def turn_bank(dtype=F32):
-            turn[0] += 1
-            return bank("t%d" % (turn[0] % 2), dtype)
+            nc.scalar.activation(out=u_sb[:, c], in_=a_sb[:, c], func=ACT.Tanh)
 
         phi_tok, phi_k, codes, scales = {}, {}, {}, {}
 
-        def products(n, hf):
-            c, g = divmod(n, PASSES)
-            if hf == 0:
-                phi_tok[n] = work.tile([P, TT, 2, 256], BF16, name="phi_tok", tag="phi_tok")
-            for t in (2 * hf, 2 * hf + 1):
-                for ii in range(8):
-                    i = 8 * g + ii
-                    lam_i = lam_ps[i // 16][:].bitcast(BF16)[:, 64 * (i % 16) : 64 * (i % 16 + 1)]
-                    nc.vector.scalar_tensor_tensor(
-                        out=phi_tok[n][:, t, :, 32 * ii : 32 * (ii + 1)],
-                        in0=lam_i.rearrange("m (u x) -> m u x", u=2),
-                        scalar=u_sb[:, c, I * t + i : I * t + i + 1],
-                        in1=v_sb[:, c, :, t, :],
-                        op0=ALU.mult,
-                        op1=ALU.mult,
-                    )
+        def lam_of(i):
+            lam_i = lam_ps[i // 16][:].bitcast(BF16)[:, 64 * (i % 16) : 64 * (i % 16 + 1)]
+            return lam_i.rearrange("m (u x) -> m u x", u=2)
 
-        def turn_phi(n, hf):
+        def products(c, t, g):
+            unit, slot = ((c, t), g) if c == 0 else ((c, g), t)
+            if slot == 0:
+                phi_tok[unit] = work.tile([P, 2, 4, 256], BF16, name="phi_tok", tag="phi_tok", bufs=4)
+            for ii in range(8):
+                i = 8 * g + ii
+                nc.vector.scalar_tensor_tensor(
+                    out=phi_tok[unit][:, :, slot, 32 * ii : 32 * (ii + 1)],
+                    in0=lam_of(i),
+                    scalar=u_sb[:, c, t, i : i + 1],
+                    in1=v_sb[:, c, :, t, :],
+                    op0=ALU.mult,
+                    op1=ALU.mult,
+                )
+
+        def turn_phi(unit, hf):
             if hf == 0:
-                phi_k[n] = work.tile([P, CHUNK * 4], BF16, name="phi_k", tag="phi_k", align_bytes=64)
+                phi_k[unit] = work.tile([P, 2048], BF16, name="phi_k", tag="phi_k", align_bytes=64, bufs=4)
             ps = turn_bank()
             for s in range(2):
                 for u in range(2):
                     nc.tensor.transpose(
                         ps[:, P * (2 * s + u) : P * (2 * s + u + 1)],
-                        phi_tok[n][:, 2 * hf + s, u, :].bitcast(F32),
+                        phi_tok[unit][:, u, 2 * hf + s, :].bitcast(F32),
                         ident[:],
                     )
             nc.scalar.copy(
-                out=phi_k[n][:, 1024 * hf : 1024 * (hf + 1)].bitcast(F32).rearrange("p (s m u) -> p s m u", s=2, u=2),
+                out=phi_k[unit][:, 1024 * hf : 1024 * (hf + 1)].bitcast(F32).rearrange("p (s m u) -> p s m u", s=2, u=2),
                 in_=ps[:].rearrange("p (s u m) -> p s m u", s=2, u=2),
             )
 
-        def quantize_phi(n):
+        for n in range(CHUNKS * PASSES):
             codes[n] = keep.tile([P, CHUNK], U32, name="codes%d" % n, align_bytes=64)
             scales[n] = keep.tile([P, CHUNK], U8, name="scales%d" % n, align_bytes=64)
-            nc.vector.quantize_mx(out=codes[n][:].bitcast(FP8X4), scales=scales[n][:], in_=phi_k[n][:])
+
+        def quantize_tile(t, g):
+            nc.vector.quantize_mx(
+                out=codes[g][:, P * t : P * (t + 1)].bitcast(FP8X4),
+                scales=scales[g][:, P * t : P * (t + 1)],
+                in_=phi_k[(0, t)][:, 512 * g : 512 * (g + 1)],
+            )
+
+        def quantize_pass(g):
+            n = PASSES + g
+            nc.vector.quantize_mx(out=codes[n][:].bitcast(FP8X4), scales=scales[n][:], in_=phi_k[(1, g)][:])
 
         acc = {}
 
-        def mx_pass(c, j, g, tag):
-            if g == 0:
-                acc[(c, j)] = bank(tag)
+        def mx_pass(dst, c, j, g, lo, hi):
             n = PASSES * c + g
             nc.tensor.matmul_mx(
-                out=acc[(c, j)][:],
+                out=dst,
                 lhsT=w_words[:, g, 2 * P * j : 2 * P * (j + 1)].bitcast(FP4X4),
                 lhsT_scale=w_scales[:, g, P * j : P * (j + 1)],
-                rhs=codes[n][:].bitcast(FP8X4),
-                rhs_scale=scales[n][:],
+                rhs=codes[n][:, lo:hi].bitcast(FP8X4),
+                rhs_scale=scales[n][:, lo:hi],
                 start=(g == 0),
                 stop=(g == PASSES - 1),
             )
+
+        def mx_wide(c, j, tag, g0=0, g1=PASSES):
+            if g0 == 0:
+                acc[(c, j)] = bank(tag)
+            for g in range(g0, g1):
+                mx_pass(acc[(c, j)][:], c, j, g, 0, CHUNK)
+
+        def mx_narrow(c, t, tiles, tag):
+            acc[(c, t, tiles)] = bank(tag)
+            for s, j in enumerate(tiles):
+                for g in range(PASSES):
+                    mx_pass(acc[(c, t, tiles)][:, P * s : P * (s + 1)], c, j, g, P * t, P * (t + 1))
 
         cols = keep.tile([P, 2 * FT], F32)
 
@@ -178,167 +209,284 @@ def tile_tucker_fusion_planes_g4_kernel(
 
         bounded, gained = {}, {}
 
+        def new_bounded(c, j):
+            bounded[(c, j)] = work.tile([P, CHUNK], F32, name="bounded", tag="bounded", bufs=10)
+
         def bound(c, j):
-            bounded[(c, j)] = work.tile([P, CHUNK], F32, name="bounded", tag="bounded", bufs=4)
+            new_bounded(c, j)
             nc.scalar.activation(out=bounded[(c, j)][:], in_=acc[(c, j)][:], func=ACT.Tanh, bias=cols[:, j : j + 1])
 
-        def gain(c, j, engine):
-            gained[(c, j)] = work.tile([P, CHUNK], F32, name="gained", tag="gained", bufs=14)
+        def bound_narrow(c, t, tiles):
+            for s, j in enumerate(tiles):
+                if t == 0:
+                    new_bounded(c, j)
+                nc.scalar.activation(
+                    out=bounded[(c, j)][:, P * t : P * (t + 1)],
+                    in_=acc[(c, t, tiles)][:, P * s : P * (s + 1)],
+                    func=ACT.Tanh,
+                    bias=cols[:, j : j + 1],
+                )
+
+        def gain(c, j, engine, lo=0, hi=CHUNK):
+            if lo == 0:
+                gained[(c, j)] = work.tile([P, CHUNK], F32, name="gained", tag="gained", bufs=14)
             g_col = cols[:, FT + j : FT + j + 1]
+            dst, src = gained[(c, j)][:, lo:hi], bounded[(c, j)][:, lo:hi]
             if engine == "scalar":
-                nc.scalar.activation(out=gained[(c, j)][:], in_=bounded[(c, j)][:], func=ACT.Copy, scale=g_col)
+                nc.scalar.activation(out=dst, in_=src, func=ACT.Copy, scale=g_col)
             else:
                 eng = nc.vector if engine == "vector" else nc.gpsimd
-                eng.tensor_scalar(
-                    out=gained[(c, j)][:], in0=bounded[(c, j)][:], scalar1=g_col, scalar2=0.0,
-                    op0=ALU.mult, op1=ALU.add,
-                )
+                eng.tensor_scalar(out=dst, in0=src, scalar1=g_col, scalar2=0.0, op0=ALU.mult, op1=ALU.add)
 
         y, y_pairs, y_k = {}, {}, {}
         back = {}
 
-        def turn_gained(c, j, tag):
-            back[(c, j)] = bank(tag)
-            for t in range(TT):
+        def turn_gained(c, j, tag, t0=0, t1=TT):
+            back[(c, j, t0)] = bank(tag)
+            for t in range(t0, t1):
                 nc.tensor.transpose(
-                    back[(c, j)][:, P * t : P * (t + 1)], gained[(c, j)][:, P * t : P * (t + 1)], ident[:]
+                    back[(c, j, t0)][:, P * t : P * (t + 1)], gained[(c, j)][:, P * t : P * (t + 1)], ident[:]
                 )
 
-        def add_stream(c, j):
+        def add_stream(c, j, t0=0, t1=TT):
             f, jj = divmod(j, 4)
             if jj == 0:
                 y[(c, f)] = work.tile([P, TT, 512], F32, name="y", tag="y", bufs=4)
             nc.vector.tensor_tensor(
-                out=y[(c, f)][:, :, P * jj : P * (jj + 1)],
-                in0=back[(c, j)][:].rearrange("m (t p) -> m t p", t=TT),
-                in1=h_sb[:, c, :, P * j : P * (j + 1)],
+                out=y[(c, f)][:, t0:t1, P * jj : P * (jj + 1)],
+                in0=back[(c, j, t0)][:].rearrange("m (t p) -> m t p", t=TT)[:, t0:t1, :],
+                in1=h_sb[:, c, t0:t1, P * j : P * (j + 1)],
                 op=ALU.add,
             )
 
-        def store_y(c, f, lo, hi):
-            dst = out_0[CHUNK * c : CHUNK * (c + 1), 512 * f + lo : 512 * f + hi]
-            nc.sync.dma_start(out=dst.rearrange("(m t) n -> m t n", t=TT), in_=y[(c, f)][:, :, lo:hi])
+        def turn_narrow(c, t, tiles, tag):
+            back[(c, t, tiles)] = bank(tag)
+            for s, j in enumerate(tiles):
+                nc.tensor.transpose(
+                    back[(c, t, tiles)][:, P * s : P * (s + 1)], gained[(c, j)][:, P * t : P * (t + 1)], ident[:]
+                )
 
-        def round_y(c, f, lo, hi):
-            if lo == 0:
-                y_pairs[(c, f)] = work.tile([P, 2, TT, 256], BF16, name="y_pairs", tag="y_pairs")
-            nc.vector.tensor_copy(
-                out=y_pairs[(c, f)][:, :, :, lo // 2 : hi // 2].rearrange("m u t (p e) -> m u t p e", e=2),
-                in_=y[(c, f)][:, :, lo:hi].rearrange("m t (p u e) -> m u t p e", u=2, e=2),
+        def add_narrow(c, t, tiles):
+            f, jj = divmod(tiles[0], 4)
+            n = len(tiles)
+            nc.vector.tensor_tensor(
+                out=y[(c, f)][:, t, P * jj : P * (jj + n)],
+                in0=back[(c, t, tiles)][:, 0 : P * n],
+                in1=h_sb[:, c, t, P * tiles[0] : P * (tiles[0] + n)],
+                op=ALU.add,
             )
 
-        def turn_y(c, f, engines):
-            y_k[(c, f)] = work.tile([P, CHUNK * 4], BF16, name="y_k", tag="y_k", align_bytes=64)
-            words = y_k[(c, f)][:].bitcast(F32).rearrange("p (m t u) -> p m t u", t=TT, u=2)
-            for hf in range(2):
-                ps = turn_bank()
-                for s in range(2):
-                    for u in range(2):
-                        nc.tensor.transpose(
-                            ps[:, P * (2 * s + u) : P * (2 * s + u + 1)],
-                            y_pairs[(c, f)][:, u, 2 * hf + s, :].bitcast(F32),
-                            ident[:],
-                        )
-                dst = words[:, :, 2 * hf : 2 * hf + 2, :]
-                src = ps[:].rearrange("p (s u m) -> p m s u", s=2, u=2)
-                if engines[hf] == "scalar":
-                    nc.scalar.copy(out=dst, in_=src)
-                else:
-                    nc.vector.tensor_copy(out=dst, in_=src)
+        def store_y(c, f, lo=0, hi=512, t0=0, t1=TT):
+            dst = tokens(out_0, c)[:, t0:t1, 512 * f + lo : 512 * f + hi]
+            nc.sync.dma_start(out=dst, in_=y[(c, f)][:, t0:t1, lo:hi])
+
+        def round_y(c, f, engine, lo=0, hi=512, t0=0, t1=TT):
+            if lo == 0 and t0 == 0:
+                y_pairs[(c, f)] = work.tile([P, 2, TT, 256], BF16, name="y_pairs", tag="y_pairs")
+            if engine == "gpsimd":
+                nc.gpsimd.tensor_scalar(
+                    out=y_pairs[(c, f)][:].rearrange("m u t (p e) -> m u (t p) e", e=2),
+                    in0=y[(c, f)][:].rearrange("m t (p u e) -> m u (t p) e", u=2, e=2),
+                    scalar1=1.0, scalar2=0.0, op0=ALU.mult, op1=ALU.add,
+                )
+                return
+            dst = y_pairs[(c, f)][:, :, t0:t1, lo // 2 : hi // 2].rearrange("m u t (p e) -> m u t p e", e=2)
+            src = y[(c, f)][:, t0:t1, lo:hi].rearrange("m t (p u e) -> m u t p e", u=2, e=2)
+            if engine == "scalar":
+                nc.scalar.copy(out=dst, in_=src)
+            else:
+                nc.vector.tensor_copy(out=dst, in_=src)
+
+        def turn_y(c, f, t0, t1, engine, tag=None):
+            if t0 == 0:
+                y_k[(c, f)] = work.tile([P, CHUNK * 4], BF16, name="y_k", tag="y_k", align_bytes=64)
+            words = y_k[(c, f)][:].bitcast(F32)
+            ps = turn_bank() if tag is None else bank(tag)
+            for s in range(t1 - t0):
+                for u in range(2):
+                    nc.tensor.transpose(
+                        ps[:, P * (2 * s + u) : P * (2 * s + u + 1)],
+                        y_pairs[(c, f)][:, u, t0 + s, :].bitcast(F32),
+                        ident[:],
+                    )
+            src = ps[:, 0 : 2 * P * (t1 - t0)]
+            if c == 0:
+                dst = words.rearrange("p (m t u) -> p m t u", t=TT, u=2)[:, :, t0:t1, :]
+                src = src.rearrange("p (s u m) -> p m s u", u=2, m=P)
+            else:
+                dst = words.rearrange("p (t m u) -> p t m u", t=TT, u=2)[:, t0:t1]
+                src = src.rearrange("p (s u m) -> p s m u", u=2, m=P)
+            if engine == "scalar":
+                nc.scalar.copy(out=dst, in_=src)
+            else:
+                nc.vector.tensor_copy(out=dst, in_=src)
 
         y_scales = keep.tile([P, FG, M], U8, align_bytes=64)
+        y_codes = {}
 
-        def quantize_y(c, f):
-            y_codes = work.tile([P, CHUNK], U32, name="y_codes", tag="y_codes", align_bytes=64)
+        def quantize_y(c, f, lo=0, hi=CHUNK):
+            if lo == 0:
+                y_codes[(c, f)] = work.tile([P, CHUNK], U32, name="y_codes", tag="y_codes", align_bytes=64)
             nc.vector.quantize_mx(
-                out=y_codes[:].bitcast(FP8X4),
-                scales=y_scales[:, f, CHUNK * c : CHUNK * (c + 1)],
-                in_=y_k[(c, f)][:],
+                out=y_codes[(c, f)][:, lo:hi].bitcast(FP8X4),
+                scales=y_scales[:, f, CHUNK * c + lo : CHUNK * c + hi],
+                in_=y_k[(c, f)][:, 4 * lo : 4 * hi],
             )
-            dst = out_1[f].rearrange("p m t -> p (m t)")[:, 4 * CHUNK * c : 4 * CHUNK * (c + 1)]
-            nc.sync.dma_start(out=dst.bitcast(I32), in_=y_codes[:].bitcast(I32))
 
-        early = ("x0", "x1", "x2", "x3")
-        for n in range(PASSES + 1):
-            products(n, 0)
-            if n < PASSES:
-                turn_phi(n, 0)
-            if n > 0:
-                quantize_phi(n - 1)
-                for j in range(4):
-                    mx_pass(0, j, n - 1, early[j])
-            if n == 2:
-                turn_rows()
-            if n < PASSES:
-                products(n, 1)
-                turn_phi(n, 1)
-        for j in range(4):
-            bound(0, j)
+        def store_codes(c, f, lo=0, hi=CHUNK, eng=nc.sync):
+            dst = out_1[f].rearrange("p m t -> p (m t)")[:, 4 * (CHUNK * c + lo) : 4 * (CHUNK * c + hi)]
+            eng.dma_start(out=dst.bitcast(I32), in_=y_codes[(c, f)][:, lo:hi].bitcast(I32))
+
+        def store_scales(c, engines):
+            for q in range(4):
+                engines[q].dma_start(
+                    out=out_2[:, 4 * q : 4 * q + 4, CHUNK * c : CHUNK * (c + 1)].rearrange("f r m -> r f m").bitcast(I32),
+                    in_=y_scales[32 * q : 32 * q + 4, :, CHUNK * c : CHUNK * (c + 1)].bitcast(I32),
+                )
+
+        early = ((0, 1, 2), (3, 4, 5))
+
+        def narrow(t, tiles, tag):
+            mx_narrow(0, t, tiles, tag)
+            bound_narrow(0, t, tiles)
+
+        factors(0)
+        products(0, 0, 0)
+        products(0, 0, 1)
+        turn_phi((0, 0), 0)
+        products(0, 0, 2)
+        products(0, 0, 3)
+        turn_phi((0, 0), 1)
+        turn_rows()
+        factors(1)
+        for t in range(TT):
+            nxt = [(0, t + 1, g) for g in range(PASSES)] if t + 1 < TT else [(1, s, 0) for s in range(TT)]
+            unit = (0, t + 1) if t + 1 < TT else (1, 0)
+            products(*nxt[0])
+            quantize_tile(t, 0)
+            quantize_tile(t, 1)
+            products(*nxt[1])
+            quantize_tile(t, 2)
+            quantize_tile(t, 3)
+            turn_phi(unit, 0)
+            narrow(t, early[0], "x%d" % (2 * (t % 2)))
+            products(*nxt[2])
+            products(*nxt[3])
+            turn_phi(unit, 1)
+            narrow(t, early[1], "x%d" % (2 * (t % 2) + 1))
+        for j in range(6):
             gain(0, j, "gpsimd")
 
-        def mx_pair(k, engine):
-            c, kk = divmod(k, FT // 2)
-            for s in range(2):
-                for g in range(PASSES):
-                    mx_pass(c, 2 * kk + s, g, "x%d" % s)
-                bound(c, 2 * kk + s)
-            for s in range(2):
-                gain(c, 2 * kk + s, engine)
+        def wide(c, j, tag, engine="gpsimd"):
+            mx_wide(c, j, tag)
+            bound(c, j)
+            gain(c, j, engine)
 
-        for n in range(PASSES, 2 * PASSES):
-            if n > PASSES:
-                products(n, 0)
-                if n > PASSES + 1:
-                    add_stream(0, n - PASSES - 2)
-                quantize_phi(n - 1)
-            products(n, 1)
-            turn_phi(n, 0)
-            turn_phi(n, 1)
-            if n > PASSES:
-                turn_gained(0, n - PASSES - 1, "x%d" % (2 + n % 2))
-            mx_pair(n - 2, "gpsimd")
+        def pass_products(g, t0=0, t1=TT):
+            for t in range(t0, t1):
+                products(1, t, g)
+
+        for g in (1, 2, 3):
+            pass_products(g, 0, 4)
+            quantize_pass(g - 1)
+            wide(0, 4 + 2 * g, "x0")
+            wide(0, 5 + 2 * g, "x1")
+            turn_phi((1, g), 0)
+            turn_phi((1, g), 1)
+            if g == 2:
+                turn_gained(0, 0, "x2")
+            if g == 3:
+                turn_gained(0, 1, "x3")
+                turn_gained(0, 2, "l0")
+        add_stream(0, 0)
+        add_stream(0, 1)
+        quantize_pass(3)
         add_stream(0, 2)
-        quantize_phi(2 * PASSES - 1)
+        for j in range(2):
+            mx_wide(1, j, "x%d" % j, 0, 3)
+        for j in range(2):
+            mx_wide(1, j, "x%d" % j, 3, 4)
+            bound(1, j)
+            gain(1, j, "gpsimd")
 
-        back_tags = ("l0", "l1", "x2", "x3")
+        back_tags = ("l1", "x2", "x3", "l0")
         runs = [
             ([(0, 3), (0, 4), (0, 5), (0, 6)], None),
             ([(0, 7), (0, 8), (0, 9), (0, 10)], (0, 0)),
-            ([(0, 11), (1, 0), (1, 1)], (0, 1)),
-            ([(1, 2), (1, 3)], (0, 2)),
-            ([(1, 4), (1, 5)], (1, 0)),
-            ([(1, 6), (1, 7)], None),
-            ([(1, 8), (1, 9)], (1, 1)),
+            ([(0, 11), (1, 0), (1, 1), (1, 2)], (0, 1)),
+            ([(1, 3), (1, 4), (1, 5)], (0, 2)),
+            ([(1, 6), (1, 7)], (1, 0)),
         ]
         for step, (tiles, plane) in enumerate(runs):
             if step > 0:
-                mx_pair(5 + step, "scalar" if step < len(runs) - 1 else "vector")
+                wide(1, 2 * step, "x0")
+                wide(1, 2 * step + 1, "x1", "gpsimd")
             for s, (c, j) in enumerate(tiles):
                 turn_gained(c, j, back_tags[s])
             if plane is not None:
-                turn_y(plane[0], plane[1], ("scalar", "scalar"))
+                turn_y(plane[0], plane[1], 0, 2, "scalar")
+                turn_y(plane[0], plane[1], 2, 4, "scalar")
             for c, j in tiles:
                 add_stream(c, j)
-            for c, j in tiles:
                 if j % 4 == 3:
-                    round_y(c, j // 4, 0, 512)
-                    store_y(c, j // 4, 0, 512)
-            if step == len(runs) - 1:
-                round_y(1, 2, 0, 256)
-                store_y(1, 2, 0, 256)
+                    round_y(c, j // 4, "vector", 0, 512, 0, 2)
+                    round_y(c, j // 4, "scalar", 0, 512, 2, 4)
+                    store_y(c, j // 4)
             if plane is not None:
                 quantize_y(plane[0], plane[1])
-        for j in (10, 11):
-            turn_gained(1, j, back_tags[j % 4])
-        for j in (10, 11):
-            add_stream(1, j)
-        round_y(1, 2, 256, 512)
+                store_codes(plane[0], plane[1])
+            if plane == (0, 2):
+                store_scales(0, (nc.sync,) * 4)
+
+        last = (10, 11)
+
+        def tail_mx(t, tag):
+            mx_narrow(1, t, last, tag)
+            bound_narrow(1, t, last)
+            for j in last:
+                gain(1, j, "scalar", P * t, P * (t + 1))
+
+        def tail_add(t):
+            add_narrow(1, t, last)
+
+        def tail_round(t):
+            round_y(1, 2, "vector", 256, 512, t, t + 1)
+
+        def tail_q(t):
+            quantize_y(1, 2, P * t, P * (t + 1))
+
+        tail_mx(0, "x0")
+        tail_mx(1, "x1")
+        turn_gained(1, 8, "x3")
+        turn_gained(1, 9, "l0")
+        add_stream(1, 8)
+        add_stream(1, 9)
+        round_y(1, 2, "vector", 0, 256)
+        store_y(1, 2, 0, 256)
+        tail_mx(2, "l1")
+        tail_mx(3, "x2")
+        turn_narrow(1, 0, last, "x0")
+        turn_narrow(1, 1, last, "x1")
+        turn_y(1, 1, 0, 2, "scalar")
+        turn_y(1, 1, 2, 4, "scalar")
+        tail_add(0)
+        tail_add(1)
+        tail_round(0)
+        tail_round(1)
+        turn_narrow(1, 2, last, "x3")
+        turn_narrow(1, 3, last, "l0")
+        turn_y(1, 2, 0, 2, "scalar", "l1")
+        tail_add(2)
+        tail_add(3)
+        tail_round(2)
+        tail_round(3)
         store_y(1, 2, 256, 512)
-        turn_y(1, 2, ("scalar", "vector"))
-        quantize_y(1, 2)
-        for q in range(4):
-            eng = nc.sync if q % 2 == 0 else nc.scalar
-            eng.dma_start(
-                out=out_2[:, 4 * q : 4 * q + 4, :].rearrange("f r m -> r f m").bitcast(I32),
-                in_=y_scales[32 * q : 32 * q + 4, :, :].bitcast(I32),
-            )
+        quantize_y(1, 1)
+        store_codes(1, 1)
+        turn_y(1, 2, 2, 3, "scalar", "x2")
+        turn_y(1, 2, 3, 4, "scalar", "x0")
+        quantize_y(1, 2, 0, 256)
+        tail_q(2)
+        tail_q(3)
+        store_codes(1, 2)
+        store_scales(1, (nc.scalar, nc.sync, nc.scalar, nc.sync))

@@ -16,14 +16,22 @@ FP8X4 = mybir.dt.float8_e4m3fn_x4
 FP4X4 = mybir.dt.float4_e2m1fn_x4
 ACT = mybir.ActivationFunctionType
 ALU = mybir.AluOpType
+SCALAR, VECTOR, GPSIMD = "scalar", "vector", "gpsimd"
 
 P = 128
+GROUP = 512
 CHUNK = 512
 CHUNKS = M // CHUNK
-TT = CHUNK // P
-PASSES = K // 512
-FT = N // P
-FG = N // 512
+TILES = CHUNK // P
+PASSES = K // GROUP
+I_PASS = GROUP // J
+FEATURE_TILES = N // P
+FEATURE_GROUPS = N // GROUP
+TILES_PER_GROUP = GROUP // P
+
+EARLY = ((0, 1, 2), (3, 4, 5))
+LATE = (10, 11)
+AHEAD = 4
 
 
 def tile_tucker_fusion_planes_g4_kernel(
@@ -36,32 +44,39 @@ def tile_tucker_fusion_planes_g4_kernel(
         psum = ctx.enter_context(tc.psum_pool(name="psum", bufs=1))
         ctx.enter_context(tc.manual_schedule())
 
-        def bank(tag, dtype=F32):
+        ring = ["bank%d" % n for n in range(6)]
+
+        def next_bank(dtype=F32):
+            tag = ring[0]
+            ring[:] = ring[1:] + [tag]
             return psum.tile([P, 512], dtype, name=tag, tag=tag)
 
+        def join_ring(tag):
+            ring[:] = [tag] + ring
+
+        sample_order = ("(m t)", "(t m)")
+
+        def samples(ap, c):
+            return ap[CHUNK * c : CHUNK * (c + 1), :].rearrange(sample_order[c] + " n -> m t n", t=TILES)
+
         lam_rows = keep.tile([P, P], F32)
-        lam_words = keep.tile([P, 8], F32)
-        a_sb = keep.tile([P, CHUNKS, TT, I], BF16)
-        b_sb = keep.tile([P, CHUNKS, TT, J], BF16)
+        lam_pairs = keep.tile([P, K // 2 // P], F32)
+        a_sb = keep.tile([P, CHUNKS, TILES, I], BF16)
+        b_sb = keep.tile([P, CHUNKS, TILES, J], BF16)
         w_scales = keep.tile([P, PASSES, N], U8, align_bytes=64)
         w_words = keep.tile([P, PASSES, 2 * N], U8, align_bytes=64)
         rows = keep.tile([P, P], BF16)
-        h_sb = keep.tile([P, CHUNKS, TT, N], BF16)
+        h_sb = keep.tile([P, CHUNKS, TILES, N], BF16)
         warm = keep.tile([P, 1], F32)
         warm_out = keep.tile([P, 1], F32)
         ident = keep.tile([P, P], F32)
         ident_bf = keep.tile([P, P], BF16)
         perm = keep.tile([P, P], F32)
 
-        order = ("(m t)", "(t m)")
-
-        def tokens(ap, c):
-            return ap[CHUNK * c : CHUNK * (c + 1), :].rearrange(order[c] + " n -> m t n", t=TT)
-
         nc.vector.memset(lam_rows[:], 0.0)
-        nc.sync.dma_start(out=lam_rows[0:8, :], in_=lam.bitcast(F32).rearrange("(r q) -> r q", q=P))
-        nc.sync.dma_start(out=b_sb[:, 0], in_=tokens(b, 0))
-        nc.sync.dma_start(out=a_sb[:, 0], in_=tokens(a, 0))
+        nc.sync.dma_start(out=lam_rows[0 : K // 2 // P, :], in_=lam.bitcast(F32).rearrange("(r q) -> r q", q=P))
+        nc.sync.dma_start(out=b_sb[:, 0], in_=samples(b, 0))
+        nc.sync.dma_start(out=a_sb[:, 0], in_=samples(a, 0))
 
         nc.vector.memset(warm[:], 0.0)
         nc.scalar.activation(out=warm_out[:], in_=warm[:], func=ACT.Tanh)
@@ -74,255 +89,212 @@ def tile_tucker_fusion_planes_g4_kernel(
         )
         nc.vector.tensor_copy(out=ident_bf[:], in_=ident[:])
 
-        for q in range(4):
+        for quadrant in range(4):
             nc.sync.dma_start(
-                out=w_scales[32 * q : 32 * q + 4, :, :].bitcast(I32),
-                in_=core_scales[:, 4 * q : 4 * q + 4, :].rearrange("g r n -> r g n").bitcast(I32),
+                out=w_scales[32 * quadrant : 32 * quadrant + 4, :, :].bitcast(I32),
+                in_=core_scales[:, 4 * quadrant : 4 * quadrant + 4, :].rearrange("g r n -> r g n").bitcast(I32),
             )
-        for f in range(FG):
+        for f in range(FEATURE_GROUPS):
+            columns = slice(2 * GROUP * f, 2 * GROUP * (f + 1))
             nc.sync.dma_start(
-                out=w_words[:, :, 1024 * f : 1024 * (f + 1)].bitcast(I32),
-                in_=core_words[:, :, 1024 * f : 1024 * (f + 1)].rearrange("g p n -> p g n").bitcast(I32),
+                out=w_words[:, :, columns].bitcast(I32),
+                in_=core_words[:, :, columns].rearrange("g p n -> p g n").bitcast(I32),
             )
-        nc.gpsimd.dma_start(out=rows[0:FT, :], in_=beta.rearrange("(j p) -> j p", p=P))
-        nc.gpsimd.dma_start(out=rows[FT : 2 * FT, :], in_=gamma.rearrange("(j p) -> j p", p=P))
-        nc.sync.dma_start(out=b_sb[:, 1], in_=tokens(b, 1))
-        nc.sync.dma_start(out=a_sb[:, 1], in_=tokens(a, 1))
+        nc.gpsimd.dma_start(out=rows[0:FEATURE_TILES, :], in_=beta.rearrange("(j p) -> j p", p=P))
+        nc.gpsimd.dma_start(out=rows[FEATURE_TILES : 2 * FEATURE_TILES, :], in_=gamma.rearrange("(j p) -> j p", p=P))
+        nc.sync.dma_start(out=b_sb[:, 1], in_=samples(b, 1))
+        nc.sync.dma_start(out=a_sb[:, 1], in_=samples(a, 1))
         for c in range(CHUNKS):
-            nc.sync.dma_start(out=h_sb[:, c], in_=tokens(h, c))
+            nc.sync.dma_start(out=h_sb[:, c], in_=samples(h, c))
 
-        turn = [0]
-
-        def turn_bank(dtype=F32):
-            turn[0] += 1
-            return bank("t%d" % (turn[0] % 2), dtype)
-
-        ps = turn_bank()
-        nc.tensor.transpose(ps[:, 0:P], lam_rows[:], ident[:])
-        nc.vector.tensor_copy(out=lam_words[:], in_=ps[:, 0:8])
-
-        lam_ps = []
+        lam_turned = next_bank()
+        nc.tensor.transpose(lam_turned[:, 0:P], lam_rows[:], ident[:])
+        nc.vector.tensor_copy(out=lam_pairs[:], in_=lam_turned[:, 0 : K // 2 // P])
+        lam_banks = []
         for half in range(2):
-            lam_bank = bank("l%d" % half)
+            lam_bank = psum.tile([P, 512], F32, name="lam%d" % half, tag="lam%d" % half)
             for r in range(4):
-                col = 4 * half + r
-                nc.tensor.transpose(
-                    lam_bank[:, P * r : P * (r + 1)], lam_words[:, col : col + 1].to_broadcast([P, P]), perm[:]
-                )
-            lam_ps.append(lam_bank)
+                column = lam_pairs[:, 4 * half + r : 4 * half + r + 1]
+                nc.tensor.transpose(lam_bank[:, P * r : P * (r + 1)], column.to_broadcast([P, P]), perm[:])
+            lam_banks.append(lam_bank)
 
-        u_sb = keep.tile([P, CHUNKS, TT, I], F32)
-        v_sb = keep.tile([P, CHUNKS, 2, TT, 32], F32)
+        beta_gamma = keep.tile([P, 2 * FEATURE_TILES], F32)
+
+        def turn_rows():
+            turned = next_bank(BF16)
+            nc.tensor.transpose(turned[:, 0:P], rows[:], ident_bf[:])
+            nc.scalar.copy(out=beta_gamma[:], in_=turned[:, 0 : 2 * FEATURE_TILES])
+
+        u_sb = keep.tile([P, CHUNKS, TILES, I], F32)
+        v_sb = keep.tile([P, CHUNKS, 2, TILES, J // 2], F32)
 
         def factors(c):
             nc.scalar.activation(
                 out=v_sb[:, c].rearrange("m u t (c e) -> m u (t c) e", e=2),
-                in_=b_sb[:, c].rearrange("m t (x u e) -> m u (t x) e", u=2, e=2),
+                in_=b_sb[:, c].rearrange("m t (c u e) -> m u (t c) e", u=2, e=2),
                 func=ACT.Tanh,
             )
             nc.scalar.activation(out=u_sb[:, c], in_=a_sb[:, c], func=ACT.Tanh)
 
-        phi_tok, phi_k, codes, scales = {}, {}, {}, {}
+        phi_pairs, phi_k, codes, scales = {}, {}, {}, {}
+        for c in range(CHUNKS):
+            for g in range(PASSES):
+                codes[(c, g)] = keep.tile([P, CHUNK], U32, name="codes%d%d" % (c, g), align_bytes=64)
+                scales[(c, g)] = keep.tile([P, CHUNK], U8, name="scales%d%d" % (c, g), align_bytes=64)
 
-        def lam_of(i):
-            lam_i = lam_ps[i // 16][:].bitcast(BF16)[:, 64 * (i % 16) : 64 * (i % 16 + 1)]
-            return lam_i.rearrange("m (u x) -> m u x", u=2)
-
-        def products(c, t, g):
-            unit, slot = ((c, t), g) if c == 0 else ((c, g), t)
+        def products(batch, slot):
+            c = batch[0]
+            t, g = (batch[1], slot) if c == 0 else (slot, batch[1])
             if slot == 0:
-                phi_tok[unit] = work.tile([P, 2, 4, 256], BF16, name="phi_tok", tag="phi_tok", bufs=4)
-            for ii in range(8):
-                i = 8 * g + ii
+                phi_pairs[batch] = work.tile([P, 2, 4, 2 * P], BF16, name="phi_pairs", tag="phi_pairs", bufs=4)
+            for i_in in range(I_PASS):
+                half, i_half = divmod(I_PASS * g + i_in, I // 2)
+                lam_i = lam_banks[half][:].bitcast(BF16)[:, J * i_half : J * (i_half + 1)]
                 nc.vector.scalar_tensor_tensor(
-                    out=phi_tok[unit][:, :, slot, 32 * ii : 32 * (ii + 1)],
-                    in0=lam_of(i),
-                    scalar=u_sb[:, c, t, i : i + 1],
+                    out=phi_pairs[batch][:, :, slot, 32 * i_in : 32 * (i_in + 1)],
+                    in0=lam_i.rearrange("m (u x) -> m u x", u=2),
+                    scalar=u_sb[:, c, t, I_PASS * g + i_in : I_PASS * g + i_in + 1],
                     in1=v_sb[:, c, :, t, :],
                     op0=ALU.mult,
                     op1=ALU.mult,
                 )
 
-        def turn_phi(unit, hf):
-            if hf == 0:
-                phi_k[unit] = work.tile([P, 2048], BF16, name="phi_k", tag="phi_k", align_bytes=64, bufs=4)
-            ps = turn_bank()
-            for s in range(2):
+        def turn_pairs(pairs, first, count):
+            turned = next_bank()
+            for s in range(count):
                 for u in range(2):
                     nc.tensor.transpose(
-                        ps[:, P * (2 * s + u) : P * (2 * s + u + 1)],
-                        phi_tok[unit][:, u, 2 * hf + s, :].bitcast(F32),
+                        turned[:, P * (2 * s + u) : P * (2 * s + u + 1)],
+                        pairs[:, u, first + s, :].bitcast(F32),
                         ident[:],
                     )
+            return turned[:, 0 : 2 * P * count]
+
+        def turn_phi(batch, half):
+            if half == 0:
+                phi_k[batch] = work.tile([P, 4 * GROUP], BF16, name="phi_k", tag="phi_k", align_bytes=64, bufs=4)
+            turned = turn_pairs(phi_pairs[batch], 2 * half, 2)
+            dst = phi_k[batch][:, 2 * GROUP * half : 2 * GROUP * (half + 1)].bitcast(F32)
             nc.scalar.copy(
-                out=phi_k[unit][:, 1024 * hf : 1024 * (hf + 1)].bitcast(F32).rearrange("p (s m u) -> p s m u", s=2, u=2),
-                in_=ps[:].rearrange("p (s u m) -> p s m u", s=2, u=2),
+                out=dst.rearrange("p (s m u) -> p s m u", m=P, u=2),
+                in_=turned.rearrange("p (s u m) -> p s m u", m=P, u=2),
             )
 
-        for n in range(CHUNKS * PASSES):
-            codes[n] = keep.tile([P, CHUNK], U32, name="codes%d" % n, align_bytes=64)
-            scales[n] = keep.tile([P, CHUNK], U8, name="scales%d" % n, align_bytes=64)
-
-        def quantize_tile(t, g):
-            nc.vector.quantize_mx(
-                out=codes[g][:, P * t : P * (t + 1)].bitcast(FP8X4),
-                scales=scales[g][:, P * t : P * (t + 1)],
-                in_=phi_k[(0, t)][:, 512 * g : 512 * (g + 1)],
-            )
+        def quantize_tile(t):
+            for g in range(PASSES):
+                nc.vector.quantize_mx(
+                    out=codes[(0, g)][:, P * t : P * (t + 1)].bitcast(FP8X4),
+                    scales=scales[(0, g)][:, P * t : P * (t + 1)],
+                    in_=phi_k[(0, t)][:, GROUP * g : GROUP * (g + 1)],
+                )
 
         def quantize_pass(g):
-            n = PASSES + g
-            nc.vector.quantize_mx(out=codes[n][:].bitcast(FP8X4), scales=scales[n][:], in_=phi_k[(1, g)][:])
+            nc.vector.quantize_mx(out=codes[(1, g)][:].bitcast(FP8X4), scales=scales[(1, g)][:], in_=phi_k[(1, g)][:])
 
-        acc = {}
-
-        def mx_pass(dst, c, j, g, lo, hi):
-            n = PASSES * c + g
+        def mx_pass(acc, c, j, g, columns):
             nc.tensor.matmul_mx(
-                out=dst,
+                out=acc,
                 lhsT=w_words[:, g, 2 * P * j : 2 * P * (j + 1)].bitcast(FP4X4),
                 lhsT_scale=w_scales[:, g, P * j : P * (j + 1)],
-                rhs=codes[n][:, lo:hi].bitcast(FP8X4),
-                rhs_scale=scales[n][:, lo:hi],
+                rhs=codes[(c, g)][:, columns].bitcast(FP8X4),
+                rhs_scale=scales[(c, g)][:, columns],
                 start=(g == 0),
                 stop=(g == PASSES - 1),
             )
 
-        def mx_wide(c, j, tag, g0=0, g1=PASSES):
-            if g0 == 0:
-                acc[(c, j)] = bank(tag)
-            for g in range(g0, g1):
-                mx_pass(acc[(c, j)][:], c, j, g, 0, CHUNK)
+        whole = slice(0, CHUNK)
 
-        def mx_narrow(c, t, tiles, tag):
-            acc[(c, t, tiles)] = bank(tag)
-            for s, j in enumerate(tiles):
-                for g in range(PASSES):
-                    mx_pass(acc[(c, t, tiles)][:, P * s : P * (s + 1)], c, j, g, P * t, P * (t + 1))
-
-        cols = keep.tile([P, 2 * FT], F32)
-
-        def turn_rows():
-            ps = turn_bank(BF16)
-            nc.tensor.transpose(ps[:, 0:P], rows[:], ident_bf[:])
-            nc.scalar.copy(out=cols[:], in_=ps[:, 0 : 2 * FT])
+        def tile_columns(t):
+            return slice(P * t, P * (t + 1))
 
         bounded, gained = {}, {}
 
-        def new_bounded(c, j):
-            bounded[(c, j)] = work.tile([P, CHUNK], F32, name="bounded", tag="bounded", bufs=10)
+        def bound(c, j, acc, columns):
+            if columns.start == 0:
+                bounded[(c, j)] = work.tile([P, CHUNK], F32, name="bounded", tag="bounded", bufs=10)
+            nc.scalar.activation(
+                out=bounded[(c, j)][:, columns], in_=acc, func=ACT.Tanh, bias=beta_gamma[:, j : j + 1]
+            )
 
-        def bound(c, j):
-            new_bounded(c, j)
-            nc.scalar.activation(out=bounded[(c, j)][:], in_=acc[(c, j)][:], func=ACT.Tanh, bias=cols[:, j : j + 1])
-
-        def bound_narrow(c, t, tiles):
-            for s, j in enumerate(tiles):
-                if t == 0:
-                    new_bounded(c, j)
-                nc.scalar.activation(
-                    out=bounded[(c, j)][:, P * t : P * (t + 1)],
-                    in_=acc[(c, t, tiles)][:, P * s : P * (s + 1)],
-                    func=ACT.Tanh,
-                    bias=cols[:, j : j + 1],
-                )
-
-        def gain(c, j, engine, lo=0, hi=CHUNK):
-            if lo == 0:
+        def gain(c, j, engine, columns=whole):
+            if columns.start == 0:
                 gained[(c, j)] = work.tile([P, CHUNK], F32, name="gained", tag="gained", bufs=14)
-            g_col = cols[:, FT + j : FT + j + 1]
-            dst, src = gained[(c, j)][:, lo:hi], bounded[(c, j)][:, lo:hi]
-            if engine == "scalar":
-                nc.scalar.activation(out=dst, in_=src, func=ACT.Copy, scale=g_col)
+            gamma_j = beta_gamma[:, FEATURE_TILES + j : FEATURE_TILES + j + 1]
+            dst, src = gained[(c, j)][:, columns], bounded[(c, j)][:, columns]
+            if engine == SCALAR:
+                nc.scalar.activation(out=dst, in_=src, func=ACT.Copy, scale=gamma_j)
             else:
-                eng = nc.vector if engine == "vector" else nc.gpsimd
-                eng.tensor_scalar(out=dst, in0=src, scalar1=g_col, scalar2=0.0, op0=ALU.mult, op1=ALU.add)
+                on = nc.vector if engine == VECTOR else nc.gpsimd
+                on.tensor_scalar(out=dst, in0=src, scalar1=gamma_j, scalar2=0.0, op0=ALU.mult, op1=ALU.add)
 
-        y, y_pairs, y_k = {}, {}, {}
-        back = {}
+        def multiply_chunk(c, j, gain_engine):
+            acc = next_bank()
+            for g in range(PASSES):
+                mx_pass(acc[:], c, j, g, whole)
+            bound(c, j, acc[:], whole)
+            gain(c, j, gain_engine)
 
-        def turn_gained(c, j, tag, t0=0, t1=TT):
-            back[(c, j, t0)] = bank(tag)
-            for t in range(t0, t1):
-                nc.tensor.transpose(
-                    back[(c, j, t0)][:, P * t : P * (t + 1)], gained[(c, j)][:, P * t : P * (t + 1)], ident[:]
-                )
+        def multiply_tile(c, t, feature_tiles):
+            acc = next_bank()
+            for s, j in enumerate(feature_tiles):
+                for g in range(PASSES):
+                    mx_pass(acc[:, P * s : P * (s + 1)], c, j, g, tile_columns(t))
+            for s, j in enumerate(feature_tiles):
+                bound(c, j, acc[:, P * s : P * (s + 1)], tile_columns(t))
 
-        def add_stream(c, j, t0=0, t1=TT):
-            f, jj = divmod(j, 4)
-            if jj == 0:
-                y[(c, f)] = work.tile([P, TT, 512], F32, name="y", tag="y", bufs=4)
+        back, y, y_pairs, y_k, y_codes = {}, {}, {}, {}, {}
+        y_scales = keep.tile([P, FEATURE_GROUPS, M], U8, align_bytes=64)
+
+        def turn_back(c, j):
+            back[(c, j)] = next_bank()
+            for t in range(TILES):
+                nc.tensor.transpose(back[(c, j)][:, tile_columns(t)], gained[(c, j)][:, tile_columns(t)], ident[:])
+
+        def add_stream(c, j):
+            f, j_in = divmod(j, TILES_PER_GROUP)
+            if j_in == 0:
+                y[(c, f)] = work.tile([P, TILES, GROUP], F32, name="y", tag="y", bufs=4)
             nc.vector.tensor_tensor(
-                out=y[(c, f)][:, t0:t1, P * jj : P * (jj + 1)],
-                in0=back[(c, j, t0)][:].rearrange("m (t p) -> m t p", t=TT)[:, t0:t1, :],
-                in1=h_sb[:, c, t0:t1, P * j : P * (j + 1)],
+                out=y[(c, f)][:, :, P * j_in : P * (j_in + 1)],
+                in0=back[(c, j)][:].rearrange("m (t p) -> m t p", t=TILES),
+                in1=h_sb[:, c, :, P * j : P * (j + 1)],
                 op=ALU.add,
             )
 
-        def turn_narrow(c, t, tiles, tag):
-            back[(c, t, tiles)] = bank(tag)
-            for s, j in enumerate(tiles):
-                nc.tensor.transpose(
-                    back[(c, t, tiles)][:, P * s : P * (s + 1)], gained[(c, j)][:, P * t : P * (t + 1)], ident[:]
-                )
-
-        def add_narrow(c, t, tiles):
-            f, jj = divmod(tiles[0], 4)
-            n = len(tiles)
-            nc.vector.tensor_tensor(
-                out=y[(c, f)][:, t, P * jj : P * (jj + n)],
-                in0=back[(c, t, tiles)][:, 0 : P * n],
-                in1=h_sb[:, c, t, P * tiles[0] : P * (tiles[0] + n)],
-                op=ALU.add,
-            )
-
-        def store_y(c, f, lo=0, hi=512, t0=0, t1=TT):
-            dst = tokens(out_0, c)[:, t0:t1, 512 * f + lo : 512 * f + hi]
+        def store_y(c, f, lo=0, hi=GROUP, t0=0, t1=TILES):
+            dst = samples(out_0, c)[:, t0:t1, GROUP * f + lo : GROUP * f + hi]
             nc.sync.dma_start(out=dst, in_=y[(c, f)][:, t0:t1, lo:hi])
 
-        def round_y(c, f, engine, lo=0, hi=512, t0=0, t1=TT):
+        def copy(engine, out, in_):
+            if engine == SCALAR:
+                nc.scalar.copy(out=out, in_=in_)
+            else:
+                nc.vector.tensor_copy(out=out, in_=in_)
+
+        def round_y(c, f, engine, lo=0, hi=GROUP, t0=0, t1=TILES):
             if lo == 0 and t0 == 0:
-                y_pairs[(c, f)] = work.tile([P, 2, TT, 256], BF16, name="y_pairs", tag="y_pairs")
-            if engine == "gpsimd":
-                nc.gpsimd.tensor_scalar(
-                    out=y_pairs[(c, f)][:].rearrange("m u t (p e) -> m u (t p) e", e=2),
-                    in0=y[(c, f)][:].rearrange("m t (p u e) -> m u (t p) e", u=2, e=2),
-                    scalar1=1.0, scalar2=0.0, op0=ALU.mult, op1=ALU.add,
-                )
-                return
-            dst = y_pairs[(c, f)][:, :, t0:t1, lo // 2 : hi // 2].rearrange("m u t (p e) -> m u t p e", e=2)
-            src = y[(c, f)][:, t0:t1, lo:hi].rearrange("m t (p u e) -> m u t p e", u=2, e=2)
-            if engine == "scalar":
-                nc.scalar.copy(out=dst, in_=src)
-            else:
-                nc.vector.tensor_copy(out=dst, in_=src)
+                y_pairs[(c, f)] = work.tile([P, 2, TILES, 2 * P], BF16, name="y_pairs", tag="y_pairs")
+            copy(
+                engine,
+                y_pairs[(c, f)][:, :, t0:t1, lo // 2 : hi // 2].rearrange("m u t (p e) -> m u t p e", e=2),
+                y[(c, f)][:, t0:t1, lo:hi].rearrange("m t (p u e) -> m u t p e", u=2, e=2),
+            )
 
-        def turn_y(c, f, t0, t1, engine, tag=None):
+        def turn_y(c, f, t0, count, engine):
             if t0 == 0:
-                y_k[(c, f)] = work.tile([P, CHUNK * 4], BF16, name="y_k", tag="y_k", align_bytes=64)
-            words = y_k[(c, f)][:].bitcast(F32)
-            ps = turn_bank() if tag is None else bank(tag)
-            for s in range(t1 - t0):
-                for u in range(2):
-                    nc.tensor.transpose(
-                        ps[:, P * (2 * s + u) : P * (2 * s + u + 1)],
-                        y_pairs[(c, f)][:, u, t0 + s, :].bitcast(F32),
-                        ident[:],
-                    )
-            src = ps[:, 0 : 2 * P * (t1 - t0)]
+                y_k[(c, f)] = work.tile([P, 4 * CHUNK], BF16, name="y_k", tag="y_k", align_bytes=64)
+            turned = turn_pairs(y_pairs[(c, f)], t0, count)
+            dst = y_k[(c, f)][:].bitcast(F32)
             if c == 0:
-                dst = words.rearrange("p (m t u) -> p m t u", t=TT, u=2)[:, :, t0:t1, :]
-                src = src.rearrange("p (s u m) -> p m s u", u=2, m=P)
+                dst = dst.rearrange("p (m t u) -> p m t u", t=TILES, u=2)[:, :, t0 : t0 + count, :]
+                copy(engine, dst, turned.rearrange("p (t u m) -> p m t u", u=2, m=P))
             else:
-                dst = words.rearrange("p (t m u) -> p t m u", t=TT, u=2)[:, t0:t1]
-                src = src.rearrange("p (s u m) -> p s m u", u=2, m=P)
-            if engine == "scalar":
-                nc.scalar.copy(out=dst, in_=src)
-            else:
-                nc.vector.tensor_copy(out=dst, in_=src)
+                dst = dst.rearrange("p (t m u) -> p t m u", t=TILES, u=2)[:, t0 : t0 + count]
+                copy(engine, dst, turned.rearrange("p (t u m) -> p t m u", u=2, m=P))
 
-        y_scales = keep.tile([P, FG, M], U8, align_bytes=64)
-        y_codes = {}
+        def turn_plane(c, f):
+            turn_y(c, f, 0, 2, SCALAR)
+            turn_y(c, f, 2, 2, SCALAR)
 
         def quantize_y(c, f, lo=0, hi=CHUNK):
             if lo == 0:
@@ -333,160 +305,171 @@ def tile_tucker_fusion_planes_g4_kernel(
                 in_=y_k[(c, f)][:, 4 * lo : 4 * hi],
             )
 
-        def store_codes(c, f, lo=0, hi=CHUNK, eng=nc.sync):
-            dst = out_1[f].rearrange("p m t -> p (m t)")[:, 4 * (CHUNK * c + lo) : 4 * (CHUNK * c + hi)]
-            eng.dma_start(out=dst.bitcast(I32), in_=y_codes[(c, f)][:, lo:hi].bitcast(I32))
+        def store_codes(c, f, lo=0, hi=CHUNK):
+            dst = out_1[f].rearrange("p m q -> p (m q)")[:, 4 * (CHUNK * c + lo) : 4 * (CHUNK * c + hi)]
+            nc.sync.dma_start(out=dst.bitcast(I32), in_=y_codes[(c, f)][:, lo:hi].bitcast(I32))
 
-        def store_scales(c, engines):
-            for q in range(4):
-                engines[q].dma_start(
-                    out=out_2[:, 4 * q : 4 * q + 4, CHUNK * c : CHUNK * (c + 1)].rearrange("f r m -> r f m").bitcast(I32),
-                    in_=y_scales[32 * q : 32 * q + 4, :, CHUNK * c : CHUNK * (c + 1)].bitcast(I32),
+        def finish_plane(c, f):
+            quantize_y(c, f)
+            store_codes(c, f)
+
+        def store_scales(c, queues):
+            columns = slice(CHUNK * c, CHUNK * (c + 1))
+            for quadrant in range(4):
+                queues[quadrant % len(queues)].dma_start(
+                    out=out_2[:, 4 * quadrant : 4 * quadrant + 4, columns].rearrange("f r m -> r f m").bitcast(I32),
+                    in_=y_scales[32 * quadrant : 32 * quadrant + 4, :, columns].bitcast(I32),
                 )
 
-        early = ((0, 1, 2), (3, 4, 5))
-
-        def narrow(t, tiles, tag):
-            mx_narrow(0, t, tiles, tag)
-            bound_narrow(0, t, tiles)
+        def finish_tile(c, j):
+            add_stream(c, j)
+            f, j_in = divmod(j, TILES_PER_GROUP)
+            if j_in == TILES_PER_GROUP - 1:
+                round_y(c, f, VECTOR, t1=TILES // 2)
+                round_y(c, f, SCALAR, t0=TILES // 2)
+                store_y(c, f)
 
         factors(0)
-        products(0, 0, 0)
-        products(0, 0, 1)
-        turn_phi((0, 0), 0)
-        products(0, 0, 2)
-        products(0, 0, 3)
-        turn_phi((0, 0), 1)
+        for half in range(2):
+            products((0, 0), 2 * half)
+            products((0, 0), 2 * half + 1)
+            turn_phi((0, 0), half)
         turn_rows()
-        factors(1)
-        for t in range(TT):
-            nxt = [(0, t + 1, g) for g in range(PASSES)] if t + 1 < TT else [(1, s, 0) for s in range(TT)]
-            unit = (0, t + 1) if t + 1 < TT else (1, 0)
-            products(*nxt[0])
-            quantize_tile(t, 0)
-            quantize_tile(t, 1)
-            products(*nxt[1])
-            quantize_tile(t, 2)
-            quantize_tile(t, 3)
-            turn_phi(unit, 0)
-            narrow(t, early[0], "x%d" % (2 * (t % 2)))
-            products(*nxt[2])
-            products(*nxt[3])
-            turn_phi(unit, 1)
-            narrow(t, early[1], "x%d" % (2 * (t % 2) + 1))
-        for j in range(6):
-            gain(0, j, "gpsimd")
+        for t in range(TILES):
+            last = t == TILES - 1
+            batch = (1, 0) if last else (0, t + 1)
+            products(batch, 0)
+            products(batch, 1)
+            quantize_tile(t)
+            turn_phi(batch, 0)
+            multiply_tile(0, t, EARLY[0])
+            products(batch, 2)
+            products(batch, 3)
+            if not last:
+                turn_phi(batch, 1)
+            multiply_tile(0, t, EARLY[1])
+            if t == 0:
+                factors(1)
+        for j in EARLY[0] + EARLY[1]:
+            gain(0, j, GPSIMD)
 
-        def wide(c, j, tag, engine="gpsimd"):
-            mx_wide(c, j, tag)
-            bound(c, j)
-            gain(c, j, engine)
-
-        def pass_products(g, t0=0, t1=TT):
-            for t in range(t0, t1):
-                products(1, t, g)
-
-        for g in (1, 2, 3):
-            pass_products(g, 0, 4)
-            quantize_pass(g - 1)
-            wide(0, 4 + 2 * g, "x0")
-            wide(0, 5 + 2 * g, "x1")
-            turn_phi((1, g), 0)
-            turn_phi((1, g), 1)
-            if g == 2:
-                turn_gained(0, 0, "x2")
-            if g == 3:
-                turn_gained(0, 1, "x3")
-                turn_gained(0, 2, "l0")
-        add_stream(0, 0)
-        add_stream(0, 1)
+        for g in (1, 2):
+            for t in range(TILES):
+                products((1, g), t)
+        for j in (6, 7, 8, 9):
+            multiply_chunk(0, j, GPSIMD)
+        join_ring("lam0")
+        turn_phi((1, 0), 1)
+        turn_phi((1, 1), 0)
+        turn_phi((1, 1), 1)
+        turn_back(0, 0)
+        turn_phi((1, 2), 0)
+        turn_phi((1, 2), 1)
+        for t in range(TILES):
+            products((1, 3), t)
+            if t == 1:
+                finish_tile(0, 0)
+        for j in (10, 11):
+            multiply_chunk(0, j, GPSIMD)
+        join_ring("lam1")
+        for g in (0, 1, 2):
+            quantize_pass(g)
+        for half in range(2):
+            turn_phi((1, 3), half)
+            turn_back(0, 1 + 2 * half)
+            turn_back(0, 2 + 2 * half)
+        finish_tile(0, 1)
+        finish_tile(0, 2)
         quantize_pass(3)
-        add_stream(0, 2)
-        for j in range(2):
-            mx_wide(1, j, "x%d" % j, 0, 3)
-        for j in range(2):
-            mx_wide(1, j, "x%d" % j, 3, 4)
-            bound(1, j)
-            gain(1, j, "gpsimd")
+        finish_tile(0, 3)
+        finish_tile(0, 4)
+        ahead = [next_bank() for j in range(AHEAD)]
+        for g in range(PASSES):
+            for j in range(AHEAD):
+                mx_pass(ahead[j][:], 1, j, g, whole)
+        for j in range(AHEAD):
+            bound(1, j, ahead[j][:], whole)
+            gain(1, j, GPSIMD)
 
-        back_tags = ("l1", "x2", "x3", "l0")
-        runs = [
-            ([(0, 3), (0, 4), (0, 5), (0, 6)], None),
-            ([(0, 7), (0, 8), (0, 9), (0, 10)], (0, 0)),
-            ([(0, 11), (1, 0), (1, 1), (1, 2)], (0, 1)),
-            ([(1, 3), (1, 4), (1, 5)], (0, 2)),
-            ([(1, 6), (1, 7)], (1, 0)),
-        ]
-        for step, (tiles, plane) in enumerate(runs):
-            if step > 0:
-                wide(1, 2 * step, "x0")
-                wide(1, 2 * step + 1, "x1", "gpsimd")
-            for s, (c, j) in enumerate(tiles):
-                turn_gained(c, j, back_tags[s])
-            if plane is not None:
-                turn_y(plane[0], plane[1], 0, 2, "scalar")
-                turn_y(plane[0], plane[1], 2, 4, "scalar")
-            for c, j in tiles:
-                add_stream(c, j)
-                if j % 4 == 3:
-                    round_y(c, j // 4, "vector", 0, 512, 0, 2)
-                    round_y(c, j // 4, "scalar", 0, 512, 2, 4)
-                    store_y(c, j // 4)
-            if plane is not None:
-                quantize_y(plane[0], plane[1])
-                store_codes(plane[0], plane[1])
-            if plane == (0, 2):
-                store_scales(0, (nc.sync,) * 4)
+        runs = (
+            (((0, 5), (0, 6), (0, 7), (0, 8)), (0, 0), ((0, 9), (0, 10))),
+            (((0, 11), (1, 0), (1, 1)), (0, 1), ()),
+            (((1, 2), (1, 3), (1, 4)), (0, 2), ((1, 5),)),
+        )
+        for step, (before, plane, after) in enumerate(runs):
+            for c, j in before:
+                turn_back(c, j)
+            turn_plane(*plane)
+            for c, j in before:
+                finish_tile(c, j)
+            for c, j in after:
+                turn_back(c, j)
+            finish_plane(*plane)
+            for c, j in after:
+                finish_tile(c, j)
+            last = step == len(runs) - 1
+            if last:
+                store_scales(0, (nc.sync,))
+            multiply_chunk(1, AHEAD + 2 * step, GPSIMD)
+            multiply_chunk(1, AHEAD + 2 * step + 1, SCALAR if last else GPSIMD)
 
-        last = (10, 11)
-
-        def tail_mx(t, tag):
-            mx_narrow(1, t, last, tag)
-            bound_narrow(1, t, last)
-            for j in last:
-                gain(1, j, "scalar", P * t, P * (t + 1))
-
-        def tail_add(t):
-            add_narrow(1, t, last)
-
-        def tail_round(t):
-            round_y(1, 2, "vector", 256, 512, t, t + 1)
-
-        def tail_q(t):
-            quantize_y(1, 2, P * t, P * (t + 1))
-
-        tail_mx(0, "x0")
-        tail_mx(1, "x1")
-        turn_gained(1, 8, "x3")
-        turn_gained(1, 9, "l0")
-        add_stream(1, 8)
+        turn_back(1, 6)
+        turn_back(1, 7)
+        turn_plane(1, 0)
+        turn_back(1, 8)
+        turn_back(1, 9)
+        for j in (6, 7, 8):
+            add_stream(1, j)
+        round_y(1, 1, VECTOR)
+        store_y(1, 1)
         add_stream(1, 9)
-        round_y(1, 2, "vector", 0, 256)
-        store_y(1, 2, 0, 256)
-        tail_mx(2, "l1")
-        tail_mx(3, "x2")
-        turn_narrow(1, 0, last, "x0")
-        turn_narrow(1, 1, last, "x1")
-        turn_y(1, 1, 0, 2, "scalar")
-        turn_y(1, 1, 2, 4, "scalar")
-        tail_add(0)
-        tail_add(1)
-        tail_round(0)
-        tail_round(1)
-        turn_narrow(1, 2, last, "x3")
-        turn_narrow(1, 3, last, "l0")
-        turn_y(1, 2, 0, 2, "scalar", "l1")
-        tail_add(2)
-        tail_add(3)
-        tail_round(2)
-        tail_round(3)
-        store_y(1, 2, 256, 512)
-        quantize_y(1, 1)
-        store_codes(1, 1)
-        turn_y(1, 2, 2, 3, "scalar", "x2")
-        turn_y(1, 2, 3, 4, "scalar", "x0")
-        quantize_y(1, 2, 0, 256)
-        tail_q(2)
-        tail_q(3)
-        store_codes(1, 2)
-        store_scales(1, (nc.scalar, nc.sync, nc.scalar, nc.sync))
+        finish_plane(1, 0)
+
+        f_last = FEATURE_GROUPS - 1
+        late_lo = P * (LATE[0] % TILES_PER_GROUP)
+        late_back = {}
+
+        def turn_back_late(t):
+            late_back[t] = next_bank()
+            for s, j in enumerate(LATE):
+                nc.tensor.transpose(late_back[t][:, P * s : P * (s + 1)], gained[(1, j)][:, tile_columns(t)], ident[:])
+
+        def add_stream_late(t):
+            nc.vector.tensor_tensor(
+                out=y[(1, f_last)][:, t, late_lo:GROUP],
+                in0=late_back[t][:, 0 : GROUP - late_lo],
+                in1=h_sb[:, 1, t, P * LATE[0] : N],
+                op=ALU.add,
+            )
+
+        gain_engines = (SCALAR, VECTOR, VECTOR, SCALAR)
+        round_engines = (VECTOR, VECTOR, VECTOR, SCALAR)
+        for t in range(TILES):
+            multiply_tile(1, t, LATE)
+            for j in LATE:
+                gain(1, j, gain_engines[t], tile_columns(t))
+            if t == 1:
+                round_y(1, f_last, VECTOR, hi=late_lo)
+                store_y(1, f_last, hi=late_lo)
+        turn_back_late(0)
+        turn_back_late(1)
+        turn_y(1, f_last - 1, 0, 2, SCALAR)
+        turn_back_late(2)
+        turn_y(1, f_last - 1, 2, 2, SCALAR)
+        turn_back_late(3)
+        for t in range(TILES + 1):
+            if t < TILES:
+                add_stream_late(t)
+            if t > 0:
+                round_y(1, f_last, round_engines[t - 1], lo=late_lo, t0=t - 1, t1=t)
+        store_y(1, f_last, lo=late_lo, t1=TILES // 2)
+        store_y(1, f_last, lo=late_lo, t0=TILES // 2)
+        turn_y(1, f_last, 0, 1, VECTOR)
+        finish_plane(1, f_last - 1)
+        for t in range(1, TILES):
+            turn_y(1, f_last, t, 1, SCALAR)
+        for t in range(TILES):
+            quantize_y(1, f_last, P * t, P * (t + 1))
+        store_codes(1, f_last, hi=CHUNK - P)
+        store_scales(1, (nc.scalar, nc.sync))
+        store_codes(1, f_last, lo=CHUNK - P)

@@ -274,11 +274,22 @@ def tile_tucker_fusion_planes_g4_kernel(
         def round_y(c, f, engine, lo=0, hi=GROUP, t0=0, t1=TILES):
             if lo == 0 and t0 == 0:
                 y_pairs[(c, f)] = work.tile([P, 2, TILES, 2 * P], BF16, name="y_pairs", tag="y_pairs")
-            copy(
-                engine,
-                y_pairs[(c, f)][:, :, t0:t1, lo // 2 : hi // 2].rearrange("m u t (p e) -> m u t p e", e=2),
-                y[(c, f)][:, t0:t1, lo:hi].rearrange("m t (p u e) -> m u t p e", u=2, e=2),
-            )
+            dst, src = y_pairs[(c, f)][:, :, t0:t1, lo // 2 : hi // 2], y[(c, f)][:, t0:t1, lo:hi]
+            if engine == GPSIMD:
+                nc.gpsimd.tensor_scalar(
+                    out=dst.rearrange("m u t (p e) -> m u (t p) e", e=2),
+                    in0=src.rearrange("m t (p u e) -> m u (t p) e", u=2, e=2),
+                    scalar1=1.0,
+                    scalar2=0.0,
+                    op0=ALU.mult,
+                    op1=ALU.add,
+                )
+            else:
+                copy(
+                    engine,
+                    dst.rearrange("m u t (p e) -> m u t p e", e=2),
+                    src.rearrange("m t (p u e) -> m u t p e", u=2, e=2),
+                )
 
         def turn_y(c, f, t0, count, engine):
             if t0 == 0:
@@ -420,13 +431,16 @@ def tile_tucker_fusion_planes_g4_kernel(
         turn_back(1, 9)
         for j in (6, 7, 8):
             add_stream(1, j)
-        round_y(1, 1, VECTOR)
+        round_y(1, 1, SCALAR, t1=TILES // 2)
+        round_y(1, 1, GPSIMD, t0=TILES // 2)
         store_y(1, 1)
         add_stream(1, 9)
         finish_plane(1, 0)
-
         f_last = FEATURE_GROUPS - 1
         late_lo = P * (LATE[0] % TILES_PER_GROUP)
+        round_y(1, f_last, VECTOR, hi=late_lo)
+        store_y(1, f_last, hi=late_lo)
+
         late_back = {}
 
         def turn_back_late(t):
@@ -448,9 +462,6 @@ def tile_tucker_fusion_planes_g4_kernel(
             multiply_tile(1, t, LATE)
             for j in LATE:
                 gain(1, j, gain_engines[t], tile_columns(t))
-            if t == 1:
-                round_y(1, f_last, VECTOR, hi=late_lo)
-                store_y(1, f_last, hi=late_lo)
         turn_back_late(0)
         turn_back_late(1)
         turn_y(1, f_last - 1, 0, 2, SCALAR)

from contextlib import ExitStack

import concourse.mybir as mybir
from concourse.masks import make_identity

M, I, J, N = 1024, 32, 64, 1536
K = I * J
FLOPS = 2 * M * K * N

F32 = mybir.dt.float32
BF16 = mybir.dt.bfloat16
I32 = mybir.dt.int32
U32 = mybir.dt.uint32
U8 = mybir.dt.uint8
FP8X4 = mybir.dt.float8_e4m3fn_x4
FP4X4 = mybir.dt.float4_e2m1fn_x4
ACT = mybir.ActivationFunctionType
ALU = mybir.AluOpType
SCALAR, VECTOR, GPSIMD = "scalar", "vector", "gpsimd"

P = 128
GROUP = 512
CHUNK = 512
CHUNKS = M // CHUNK
TILES = CHUNK // P
PASSES = K // GROUP
I_PASS = GROUP // J
FEATURE_TILES = N // P
FEATURE_GROUPS = N // GROUP
TILES_PER_GROUP = GROUP // P

EARLY = ((0, 1, 2), (3, 4, 5))
LATE = (10, 11)
AHEAD = 4


def tile_tucker_fusion_planes_g4_kernel(
    tc, a, b, lam, core_words, core_scales, beta, gamma, h, out_0, out_1, out_2
):
    nc = tc.nc
    with ExitStack() as ctx:
        keep = ctx.enter_context(tc.tile_pool(name="keep", bufs=1))
        work = ctx.enter_context(tc.tile_pool(name="work", bufs=3))
        psum = ctx.enter_context(tc.psum_pool(name="psum", bufs=1))
        ctx.enter_context(tc.manual_schedule())

        ring = ["bank%d" % n for n in range(6)]

        def next_bank(dtype=F32):
            tag = ring[0]
            ring[:] = ring[1:] + [tag]
            return psum.tile([P, 512], dtype, name=tag, tag=tag)

        def join_ring(tag):
            ring[:] = [tag] + ring

        sample_order = ("(m t)", "(t m)")

        def samples(ap, c):
            return ap[CHUNK * c : CHUNK * (c + 1), :].rearrange(sample_order[c] + " n -> m t n", t=TILES)

        lam_rows = keep.tile([P, P], F32)
        lam_pairs = keep.tile([P, K // 2 // P], F32)
        a_sb = keep.tile([P, CHUNKS, TILES, I], BF16)
        b_sb = keep.tile([P, CHUNKS, TILES, J], BF16)
        w_scales = keep.tile([P, PASSES, N], U8, align_bytes=64)
        w_words = keep.tile([P, PASSES, 2 * N], U8, align_bytes=64)
        rows = keep.tile([P, P], BF16)
        h_sb = keep.tile([P, CHUNKS, TILES, N], BF16)
        warm = keep.tile([P, 1], F32)
        warm_out = keep.tile([P, 1], F32)
        ident = keep.tile([P, P], F32)
        ident_bf = keep.tile([P, P], BF16)
        perm = keep.tile([P, P], F32)

        nc.vector.memset(lam_rows[:], 0.0)
        nc.sync.dma_start(out=lam_rows[0 : K // 2 // P, :], in_=lam.bitcast(F32).rearrange("(r q) -> r q", q=P))
        nc.sync.dma_start(out=b_sb[:, 0], in_=samples(b, 0))
        nc.sync.dma_start(out=a_sb[:, 0], in_=samples(a, 0))

        nc.vector.memset(warm[:], 0.0)
        nc.scalar.activation(out=warm_out[:], in_=warm[:], func=ACT.Tanh)
        make_identity(nc, ident[:])
        nc.vector.memset(rows[:], 0.0)
        nc.vector.memset(w_scales[:].rearrange("p g n -> p (g n)").bitcast(I32), 0)
        nc.vector.tensor_copy(
            out=perm[:].rearrange("q (i u c) -> q i u c", i=4, u=2),
            in_=ident[:].rearrange("q (i c u) -> q i u c", i=4, u=2),
        )
        nc.vector.tensor_copy(out=ident_bf[:], in_=ident[:])

        for quadrant in range(4):
            nc.sync.dma_start(
                out=w_scales[32 * quadrant : 32 * quadrant + 4, :, :].bitcast(I32),
                in_=core_scales[:, 4 * quadrant : 4 * quadrant + 4, :].rearrange("g r n -> r g n").bitcast(I32),
            )
        for f in range(FEATURE_GROUPS):
            columns = slice(2 * GROUP * f, 2 * GROUP * (f + 1))
            nc.sync.dma_start(
                out=w_words[:, :, columns].bitcast(I32),
                in_=core_words[:, :, columns].rearrange("g p n -> p g n").bitcast(I32),
            )
        nc.gpsimd.dma_start(out=rows[0:FEATURE_TILES, :], in_=beta.rearrange("(j p) -> j p", p=P))
        nc.gpsimd.dma_start(out=rows[FEATURE_TILES : 2 * FEATURE_TILES, :], in_=gamma.rearrange("(j p) -> j p", p=P))
        nc.sync.dma_start(out=b_sb[:, 1], in_=samples(b, 1))
        nc.sync.dma_start(out=a_sb[:, 1], in_=samples(a, 1))
        for c in range(CHUNKS):
            nc.sync.dma_start(out=h_sb[:, c], in_=samples(h, c))

        lam_turned = next_bank()
        nc.tensor.transpose(lam_turned[:, 0:P], lam_rows[:], ident[:])
        nc.vector.tensor_copy(out=lam_pairs[:], in_=lam_turned[:, 0 : K // 2 // P])
        lam_banks = []
        for half in range(2):
            lam_bank = psum.tile([P, 512], F32, name="lam%d" % half, tag="lam%d" % half)
            for r in range(4):
                column = lam_pairs[:, 4 * half + r : 4 * half + r + 1]
                nc.tensor.transpose(lam_bank[:, P * r : P * (r + 1)], column.to_broadcast([P, P]), perm[:])
            lam_banks.append(lam_bank)

        beta_gamma = keep.tile([P, 2 * FEATURE_TILES], F32)

        def turn_rows():
            turned = next_bank(BF16)
            nc.tensor.transpose(turned[:, 0:P], rows[:], ident_bf[:])
            nc.scalar.copy(out=beta_gamma[:], in_=turned[:, 0 : 2 * FEATURE_TILES])

        u_sb = keep.tile([P, CHUNKS, TILES, I], F32)
        v_sb = keep.tile([P, CHUNKS, 2, TILES, J // 2], F32)

        def factors(c):
            nc.scalar.activation(
                out=v_sb[:, c].rearrange("m u t (c e) -> m u (t c) e", e=2),
                in_=b_sb[:, c].rearrange("m t (c u e) -> m u (t c) e", u=2, e=2),
                func=ACT.Tanh,
            )
            nc.scalar.activation(out=u_sb[:, c], in_=a_sb[:, c], func=ACT.Tanh)

        phi_pairs, phi_k, codes, scales = {}, {}, {}, {}
        for c in range(CHUNKS):
            for g in range(PASSES):
                codes[(c, g)] = keep.tile([P, CHUNK], U32, name="codes%d%d" % (c, g), align_bytes=64)
                scales[(c, g)] = keep.tile([P, CHUNK], U8, name="scales%d%d" % (c, g), align_bytes=64)

        def products(batch, slot):
            c = batch[0]
            t, g = (batch[1], slot) if c == 0 else (slot, batch[1])
            if slot == 0:
                phi_pairs[batch] = work.tile([P, 2, 4, 2 * P], BF16, name="phi_pairs", tag="phi_pairs", bufs=4)
            for i_in in range(I_PASS):
                half, i_half = divmod(I_PASS * g + i_in, I // 2)
                lam_i = lam_banks[half][:].bitcast(BF16)[:, J * i_half : J * (i_half + 1)]
                nc.vector.scalar_tensor_tensor(
                    out=phi_pairs[batch][:, :, slot, 32 * i_in : 32 * (i_in + 1)],
                    in0=lam_i.rearrange("m (u x) -> m u x", u=2),
                    scalar=u_sb[:, c, t, I_PASS * g + i_in : I_PASS * g + i_in + 1],
                    in1=v_sb[:, c, :, t, :],
                    op0=ALU.mult,
                    op1=ALU.mult,
                )

        def turn_pairs(pairs, first, count):
            turned = next_bank()
            for s in range(count):
                for u in range(2):
                    nc.tensor.transpose(
                        turned[:, P * (2 * s + u) : P * (2 * s + u + 1)],
                        pairs[:, u, first + s, :].bitcast(F32),
                        ident[:],
                    )
            return turned[:, 0 : 2 * P * count]

        def turn_phi(batch, half):
            if half == 0:
                phi_k[batch] = work.tile([P, 4 * GROUP], BF16, name="phi_k", tag="phi_k", align_bytes=64, bufs=4)
            turned = turn_pairs(phi_pairs[batch], 2 * half, 2)
            dst = phi_k[batch][:, 2 * GROUP * half : 2 * GROUP * (half + 1)].bitcast(F32)
            nc.scalar.copy(
                out=dst.rearrange("p (s m u) -> p s m u", m=P, u=2),
                in_=turned.rearrange("p (s u m) -> p s m u", m=P, u=2),
            )

        def quantize_tile(t):
            for g in range(PASSES):
                nc.vector.quantize_mx(
                    out=codes[(0, g)][:, P * t : P * (t + 1)].bitcast(FP8X4),
                    scales=scales[(0, g)][:, P * t : P * (t + 1)],
                    in_=phi_k[(0, t)][:, GROUP * g : GROUP * (g + 1)],
                )

        def quantize_pass(g):
            nc.vector.quantize_mx(out=codes[(1, g)][:].bitcast(FP8X4), scales=scales[(1, g)][:], in_=phi_k[(1, g)][:])

        def mx_pass(acc, c, j, g, columns):
            nc.tensor.matmul_mx(
                out=acc,
                lhsT=w_words[:, g, 2 * P * j : 2 * P * (j + 1)].bitcast(FP4X4),
                lhsT_scale=w_scales[:, g, P * j : P * (j + 1)],
                rhs=codes[(c, g)][:, columns].bitcast(FP8X4),
                rhs_scale=scales[(c, g)][:, columns],
                start=(g == 0),
                stop=(g == PASSES - 1),
            )

        whole = slice(0, CHUNK)

        def tile_columns(t):
            return slice(P * t, P * (t + 1))

        bounded, gained = {}, {}

        def bound(c, j, acc, columns):
            if columns.start == 0:
                bounded[(c, j)] = work.tile([P, CHUNK], F32, name="bounded", tag="bounded", bufs=10)
            nc.scalar.activation(
                out=bounded[(c, j)][:, columns], in_=acc, func=ACT.Tanh, bias=beta_gamma[:, j : j + 1]
            )

        def gain(c, j, engine, columns=whole):
            if columns.start == 0:
                gained[(c, j)] = work.tile([P, CHUNK], F32, name="gained", tag="gained", bufs=14)
            gamma_j = beta_gamma[:, FEATURE_TILES + j : FEATURE_TILES + j + 1]
            dst, src = gained[(c, j)][:, columns], bounded[(c, j)][:, columns]
            if engine == SCALAR:
                nc.scalar.activation(out=dst, in_=src, func=ACT.Copy, scale=gamma_j)
            else:
                on = nc.vector if engine == VECTOR else nc.gpsimd
                on.tensor_scalar(out=dst, in0=src, scalar1=gamma_j, scalar2=0.0, op0=ALU.mult, op1=ALU.add)

        def multiply_chunk(c, j, gain_engine):
            acc = next_bank()
            for g in range(PASSES):
                mx_pass(acc[:], c, j, g, whole)
            bound(c, j, acc[:], whole)
            gain(c, j, gain_engine)

        def multiply_tile(c, t, feature_tiles):
            acc = next_bank()
            for s, j in enumerate(feature_tiles):
                for g in range(PASSES):
                    mx_pass(acc[:, P * s : P * (s + 1)], c, j, g, tile_columns(t))
            for s, j in enumerate(feature_tiles):
                bound(c, j, acc[:, P * s : P * (s + 1)], tile_columns(t))

        back, y, y_pairs, y_k, y_codes = {}, {}, {}, {}, {}
        y_scales = keep.tile([P, FEATURE_GROUPS, M], U8, align_bytes=64)

        def turn_back(c, j):
            back[(c, j)] = next_bank()
            for t in range(TILES):
                nc.tensor.transpose(back[(c, j)][:, tile_columns(t)], gained[(c, j)][:, tile_columns(t)], ident[:])

        def add_stream(c, j):
            f, j_in = divmod(j, TILES_PER_GROUP)
            if j_in == 0:
                y[(c, f)] = work.tile([P, TILES, GROUP], F32, name="y", tag="y", bufs=4)
            nc.vector.tensor_tensor(
                out=y[(c, f)][:, :, P * j_in : P * (j_in + 1)],
                in0=back[(c, j)][:].rearrange("m (t p) -> m t p", t=TILES),
                in1=h_sb[:, c, :, P * j : P * (j + 1)],
                op=ALU.add,
            )

        def store_y(c, f, lo=0, hi=GROUP, t0=0, t1=TILES):
            dst = samples(out_0, c)[:, t0:t1, GROUP * f + lo : GROUP * f + hi]
            nc.sync.dma_start(out=dst, in_=y[(c, f)][:, t0:t1, lo:hi])

        def copy(engine, out, in_):
            if engine == SCALAR:
                nc.scalar.copy(out=out, in_=in_)
            else:
                nc.vector.tensor_copy(out=out, in_=in_)

        def round_y(c, f, engine, lo=0, hi=GROUP, t0=0, t1=TILES):
            if lo == 0 and t0 == 0:
                y_pairs[(c, f)] = work.tile([P, 2, TILES, 2 * P], BF16, name="y_pairs", tag="y_pairs")
            dst, src = y_pairs[(c, f)][:, :, t0:t1, lo // 2 : hi // 2], y[(c, f)][:, t0:t1, lo:hi]
            if engine == GPSIMD:
                nc.gpsimd.tensor_scalar(
                    out=dst.rearrange("m u t (p e) -> m u (t p) e", e=2),
                    in0=src.rearrange("m t (p u e) -> m u (t p) e", u=2, e=2),
                    scalar1=1.0,
                    scalar2=0.0,
                    op0=ALU.mult,
                    op1=ALU.add,
                )
            else:
                copy(
                    engine,
                    dst.rearrange("m u t (p e) -> m u t p e", e=2),
                    src.rearrange("m t (p u e) -> m u t p e", u=2, e=2),
                )

        def turn_y(c, f, t0, count, engine):
            if t0 == 0:
                y_k[(c, f)] = work.tile([P, 4 * CHUNK], BF16, name="y_k", tag="y_k", align_bytes=64)
            turned = turn_pairs(y_pairs[(c, f)], t0, count)
            dst = y_k[(c, f)][:].bitcast(F32)
            if c == 0:
                dst = dst.rearrange("p (m t u) -> p m t u", t=TILES, u=2)[:, :, t0 : t0 + count, :]
                copy(engine, dst, turned.rearrange("p (t u m) -> p m t u", u=2, m=P))
            else:
                dst = dst.rearrange("p (t m u) -> p t m u", t=TILES, u=2)[:, t0 : t0 + count]
                copy(engine, dst, turned.rearrange("p (t u m) -> p t m u", u=2, m=P))

        def turn_plane(c, f):
            turn_y(c, f, 0, 2, SCALAR)
            turn_y(c, f, 2, 2, SCALAR)

        def quantize_y(c, f, lo=0, hi=CHUNK):
            if lo == 0:
                y_codes[(c, f)] = work.tile([P, CHUNK], U32, name="y_codes", tag="y_codes", align_bytes=64)
            nc.vector.quantize_mx(
                out=y_codes[(c, f)][:, lo:hi].bitcast(FP8X4),
                scales=y_scales[:, f, CHUNK * c + lo : CHUNK * c + hi],
                in_=y_k[(c, f)][:, 4 * lo : 4 * hi],
            )

        def store_codes(c, f, lo=0, hi=CHUNK):
            dst = out_1[f].rearrange("p m q -> p (m q)")[:, 4 * (CHUNK * c + lo) : 4 * (CHUNK * c + hi)]
            nc.sync.dma_start(out=dst.bitcast(I32), in_=y_codes[(c, f)][:, lo:hi].bitcast(I32))

        def finish_plane(c, f):
            quantize_y(c, f)
            store_codes(c, f)

        def store_scales(c, queues):
            columns = slice(CHUNK * c, CHUNK * (c + 1))
            for quadrant in range(4):
                queues[quadrant % len(queues)].dma_start(
                    out=out_2[:, 4 * quadrant : 4 * quadrant + 4, columns].rearrange("f r m -> r f m").bitcast(I32),
                    in_=y_scales[32 * quadrant : 32 * quadrant + 4, :, columns].bitcast(I32),
                )

        def finish_tile(c, j):
            add_stream(c, j)
            f, j_in = divmod(j, TILES_PER_GROUP)
            if j_in == TILES_PER_GROUP - 1:
                round_y(c, f, VECTOR, t1=TILES // 2)
                round_y(c, f, SCALAR, t0=TILES // 2)
                store_y(c, f)

        factors(0)
        for half in range(2):
            products((0, 0), 2 * half)
            products((0, 0), 2 * half + 1)
            turn_phi((0, 0), half)
        turn_rows()
        for t in range(TILES):
            last = t == TILES - 1
            batch = (1, 0) if last else (0, t + 1)
            products(batch, 0)
            products(batch, 1)
            quantize_tile(t)
            turn_phi(batch, 0)
            multiply_tile(0, t, EARLY[0])
            products(batch, 2)
            products(batch, 3)
            if not last:
                turn_phi(batch, 1)
            multiply_tile(0, t, EARLY[1])
            if t == 0:
                factors(1)
        for j in EARLY[0] + EARLY[1]:
            gain(0, j, GPSIMD)

        for g in (1, 2):
            for t in range(TILES):
                products((1, g), t)
        for j in (6, 7, 8, 9):
            multiply_chunk(0, j, GPSIMD)
        join_ring("lam0")
        turn_phi((1, 0), 1)
        turn_phi((1, 1), 0)
        turn_phi((1, 1), 1)
        turn_back(0, 0)
        turn_phi((1, 2), 0)
        turn_phi((1, 2), 1)
        for t in range(TILES):
            products((1, 3), t)
            if t == 1:
                finish_tile(0, 0)
        for j in (10, 11):
            multiply_chunk(0, j, GPSIMD)
        join_ring("lam1")
        for g in (0, 1, 2):
            quantize_pass(g)
        for half in range(2):
            turn_phi((1, 3), half)
            turn_back(0, 1 + 2 * half)
            turn_back(0, 2 + 2 * half)
        finish_tile(0, 1)
        finish_tile(0, 2)
        quantize_pass(3)
        finish_tile(0, 3)
        finish_tile(0, 4)
        ahead = [next_bank() for j in range(AHEAD)]
        for g in range(PASSES):
            for j in range(AHEAD):
                mx_pass(ahead[j][:], 1, j, g, whole)
        for j in range(AHEAD):
            bound(1, j, ahead[j][:], whole)
            gain(1, j, GPSIMD)

        runs = (
            (((0, 5), (0, 6), (0, 7), (0, 8)), (0, 0), ((0, 9), (0, 10))),
            (((0, 11), (1, 0), (1, 1)), (0, 1), ()),
            (((1, 2), (1, 3), (1, 4)), (0, 2), ((1, 5),)),
        )
        for step, (before, plane, after) in enumerate(runs):
            for c, j in before:
                turn_back(c, j)
            turn_plane(*plane)
            for c, j in before:
                finish_tile(c, j)
            for c, j in after:
                turn_back(c, j)
            finish_plane(*plane)
            for c, j in after:
                finish_tile(c, j)
            last = step == len(runs) - 1
            if last:
                store_scales(0, (nc.sync,))
            multiply_chunk(1, AHEAD + 2 * step, GPSIMD)
            multiply_chunk(1, AHEAD + 2 * step + 1, SCALAR if last else GPSIMD)

        turn_back(1, 6)
        turn_back(1, 7)
        turn_plane(1, 0)
        turn_back(1, 8)
        turn_back(1, 9)
        for j in (6, 7, 8):
            add_stream(1, j)
        round_y(1, 1, SCALAR, t1=TILES // 2)
        round_y(1, 1, GPSIMD, t0=TILES // 2)
        store_y(1, 1)
        add_stream(1, 9)
        finish_plane(1, 0)
        f_last = FEATURE_GROUPS - 1
        late_lo = P * (LATE[0] % TILES_PER_GROUP)
        round_y(1, f_last, VECTOR, hi=late_lo)
        store_y(1, f_last, hi=late_lo)

        late_back = {}

        def turn_back_late(t):
            late_back[t] = next_bank()
            for s, j in enumerate(LATE):
                nc.tensor.transpose(late_back[t][:, P * s : P * (s + 1)], gained[(1, j)][:, tile_columns(t)], ident[:])

        def add_stream_late(t):
            nc.vector.tensor_tensor(
                out=y[(1, f_last)][:, t, late_lo:GROUP],
                in0=late_back[t][:, 0 : GROUP - late_lo],
                in1=h_sb[:, 1, t, P * LATE[0] : N],
                op=ALU.add,
            )

        gain_engines = (SCALAR, VECTOR, VECTOR, SCALAR)
        round_engines = (VECTOR, VECTOR, VECTOR, SCALAR)
        for t in range(TILES):
            multiply_tile(1, t, LATE)
            for j in LATE:
                gain(1, j, gain_engines[t], tile_columns(t))
        turn_back_late(0)
        turn_back_late(1)
        turn_y(1, f_last - 1, 0, 2, SCALAR)
        turn_back_late(2)
        turn_y(1, f_last - 1, 2, 2, SCALAR)
        turn_back_late(3)
        for t in range(TILES + 1):
            if t < TILES:
                add_stream_late(t)
            if t > 0:
                round_y(1, f_last, round_engines[t - 1], lo=late_lo, t0=t - 1, t1=t)
        store_y(1, f_last, lo=late_lo, t1=TILES // 2)
        store_y(1, f_last, lo=late_lo, t0=TILES // 2)
        turn_y(1, f_last, 0, 1, VECTOR)
        finish_plane(1, f_last - 1)
        for t in range(1, TILES):
            turn_y(1, f_last, t, 1, SCALAR)
        for t in range(TILES):
            quantize_y(1, f_last, P * t, P * (t + 1))
        store_codes(1, f_last, hi=CHUNK - P)
        store_scales(1, (nc.scalar, nc.sync))
        store_codes(1, f_last, lo=CHUNK - P)
